import numpy as np
import ml_dtypes


def mxq(x, axis, fmt="e4m3"):
    dtype, down = {"e4m3": (ml_dtypes.float8_e4m3fn, 7), "e5m2": (ml_dtypes.float8_e5m2, 14)}[fmt]
    v = np.moveaxis(np.asarray(x, np.float32).astype(ml_dtypes.bfloat16).astype(np.float64), axis, -1)
    blocks = v.reshape(v.shape[:-1] + (-1, 32))
    amax = np.abs(blocks).max(-1, keepdims=True)
    byte = np.maximum(np.where(amax > 0, np.frexp(amax)[1] - 1 + 127, 0) - down, 1)
    scale = np.exp2(byte - 127.0)
    codes = (blocks / scale).astype(np.float32).astype(dtype).astype(np.float64)
    return np.moveaxis((codes * scale).reshape(v.shape), -1, axis)


WIDE = False


def mx_kscale(k):
    if not WIDE:
        return np.ones(k)
    levels = np.array([10, -10, 5, -5, 0])
    if k % 512:
        return np.exp2(np.random.permutation(np.resize(levels, k // 32))).repeat(32)
    a = np.empty((k // 512, 16))
    for p in range(k // 512):
        a[p, :8] = np.random.permutation(np.resize(levels, 8))
        for g in range(8):
            far = levels[np.abs(levels - a[p, g]) >= 10]
            a[p, g + 8] = far[np.random.randint(len(far))]
    return np.exp2(a.ravel()).repeat(32)


def f64(x):
    return np.asarray(x).astype(np.float64)


def striped(idx):
    return np.tile(idx.reshape(-1, 16).T, (8, 1)).astype(np.uint16)


def unstriped(offs):
    return offs[:16].T.reshape(-1).astype(np.int64)


E2M1 = np.array([0.0, 0.5, 1.0, 1.5, 2.0, 3.0, 4.0, 6.0, -0.0, -0.5, -1.0, -1.5, -2.0, -3.0, -4.0, -6.0])


def pack_weight(w, fmt):
    k, n = w.shape
    w = f64(np.asarray(w, np.float32).astype(ml_dtypes.bfloat16)).reshape(k // 32, 32, n)
    amax = np.abs(w).max(1)
    if fmt == "e4m3":
        byte = np.frexp(amax)[1] - 1 + 127 - 7
    else:
        mant, ex = np.frexp(amax / 6.0)
        byte = np.where(mant > 0.5, ex, ex - 1) + 127
    byte = np.clip(np.where(amax > 0, byte, 1), 1, 254)
    scaled = (w * np.exp2(127.0 - byte)[:, None, :]).reshape(k, n).astype(np.float32)
    by_word = np.ascontiguousarray(scaled.reshape(k // 512, 128, 4, n).transpose(0, 1, 3, 2))
    if fmt == "e4m3":
        words = by_word.astype(ml_dtypes.float8_e4m3fn).view(np.uint8)
    else:
        c = by_word.astype(ml_dtypes.float4_e2m1fn).view(np.uint8) & 0xF
        words = (c[..., 0::2] | (c[..., 1::2] << 4)).reshape(k // 512, 128, 2 * n)
    return np.ascontiguousarray(words), np.ascontiguousarray(byte.astype(np.uint8).reshape(k // 512, 16, n))


def unpack_weight(words, scales, fmt):
    g, _, n = scales.shape
    words = np.ascontiguousarray(words).reshape(g, 128, n, -1)
    if fmt == "e4m3":
        vals = words.view(ml_dtypes.float8_e4m3fn).astype(np.float64)
    else:
        nib = np.empty((g, 128, n, 4), np.uint8)
        nib[..., 0::2] = words & 0xF
        nib[..., 1::2] = words >> 4
        vals = E2M1[nib]
    vals = vals * np.repeat(np.exp2(scales.astype(np.float64) - 127.0), 8, axis=1)[..., None]
    return vals.transpose(0, 1, 3, 2).reshape(g * 512, n)


def d_relu2(v):
    return 2.0 * np.maximum(v, 0.0)


K, T, E, C, H, N = 128, 1280, 5, 256, 512, 512


def by_expert(wq, xq):
    return np.concatenate([wq[e].T @ xq[:, e * C:(e + 1) * C] for e in range(E)], axis=1)


def setup_inputs():
    n = np.random.standard_normal
    v = mx_kscale(N)
    u = mx_kscale(H)
    slot_token = np.random.permutation(T)[:E * C]
    w_slot = np.random.uniform(0.2, 1.0, E * C)
    dy = pack_weight(n((N, T)) * v[:, None], "e4m3")
    w2t = pack_weight(n((N, H)) / np.sqrt(N) / v[:, None] * u, "e2m1")
    return {
        "dy_words": dy[0],
        "dy_scales": dy[1],
        "w2t_words": w2t[0],
        "w2t_scales": w2t[1],
        "w1t": (n((E, H, K)) / np.sqrt(H) / u[None, :, None]).astype(np.float32),
        "a": (n((H, E * C))).astype(np.float32),
        "gate": (np.tile(w_slot, (128, 1))).astype(np.float32),
        "offs": striped(slot_token),
    }


def reference(dy_words, dy_scales, w2t_words, w2t_scales, w1t, a, gate, offs):
    w2t = unpack_weight(w2t_words, w2t_scales, "e2m1")
    w1tq = mxq(f64(w1t), 1, "e4m3")
    idx = unstriped(offs)
    dc = w2t.T @ unpack_weight(dy_words, dy_scales, "e4m3")
    da = f64(gate[:1]) * dc[:, idx] * d_relu2(f64(a))
    dx = by_expert(w1tq, mxq(da, 0, "e4m3"))
    out = np.zeros((K, T))
    out[:, idx] = dx
    return out

@@ -1,0 +1,232 @@
+from contextlib import ExitStack
+
+import concourse.mybir as mybir
+from concourse.masks import make_identity
+
+K, T, E, C, H, N = 128, 1280, 5, 256, 512, 512
+FLOPS = 2 * N * H * T + 2 * H * K * E * C
+
+F32 = mybir.dt.float32
+BF16 = mybir.dt.bfloat16
+I32 = mybir.dt.int32
+U32 = mybir.dt.uint32
+U16 = mybir.dt.uint16
+U8 = mybir.dt.uint8
+FP8X4 = mybir.dt.float8_e4m3fn_x4
+FP4X4 = mybir.dt.float4_e2m1fn_x4
+ACT = mybir.ActivationFunctionType
+ALU = mybir.AluOpType
+
+P = 128
+PACK = 4
+ROWS = H // P
+BLOCKS = T // P
+PER_COL = 16
+TOKEN_CUTS = ((0, 512), (512, 1024), (1024, 1280))
+CHUNKS = ((0, 512), (512, 1024), (1024, 1280))
+
+
+def tile_moe_sdb_relu2_kernel(tc, dy_words, dy_scales, w2t_words, w2t_scales, w1t, a, gate, offs, out):
+    nc = tc.nc
+    with ExitStack() as ctx:
+        keep = ctx.enter_context(tc.tile_pool(name="keep", bufs=1))
+        psum = ctx.enter_context(tc.psum_pool(name="psum", bufs=1))
+
+        offsets = keep.tile([P, T // PER_COL], U16, name="offsets")
+        dy_codes = keep.tile([P, T], U32, align_bytes=64)
+        dy_plane = keep.tile([P, T], U8, align_bytes=64)
+        w2_codes = keep.tile([P, 2 * H], U8, align_bytes=64)
+        w2_plane = keep.tile([P, H], U8, align_bytes=64)
+
+        nc.vector.memset(dy_plane[:].bitcast(I32), 0)
+        nc.gpsimd.memset(w2_plane[:].bitcast(I32), 0)
+        nc.sync.dma_start(out=w2_codes[:].bitcast(I32), in_=w2t_words[0].bitcast(I32))
+        nc.sync.dma_start(out=dy_codes[:].bitcast(I32), in_=dy_words[0].rearrange("p t d -> p (t d)").bitcast(I32))
+        for r in range(4):
+            nc.sync.dma_start(out=dy_plane[:].bitcast(I32)[r:P:32, :], in_=dy_scales[0].bitcast(I32)[r:16:4, :])
+        for r in range(4):
+            queue = nc.gpsimd if r < 2 else nc.sync
+            queue.dma_start(out=w2_plane[:].bitcast(I32)[r:P:32, :], in_=w2t_scales[0].bitcast(I32)[r:16:4, :])
+
+        a_raw = {}
+
+        def load_a(ci, t0, count):
+            lo, hi = CHUNKS[ci]
+            rows = keep.tile([P, count, hi - lo], F32, name="a_raw_%d_%d" % (ci, t0))
+            nc.sync.dma_start(out=rows[:], in_=a[P * t0 : P * (t0 + count), lo:hi].rearrange("(t p) j -> p t j", p=P))
+            for t in range(count):
+                a_raw[ci, t0 + t] = rows[:, t, :]
+
+        w1_raw = {}
+
+        def load_w1(e0, count):
+            rows = keep.tile([P, count, PACK, K], F32, name="w1_raw_%d" % e0)
+            nc.sync.dma_start(out=rows[:], in_=w1t[e0 : e0 + count].rearrange("e (p j) k -> p e j k", j=PACK))
+            for e in range(count):
+                w1_raw[e0 + e] = rows[:, e, :, :]
+
+        load_a(0, 0, 2)
+        nc.sync.dma_start(offsets[:], offs)
+        load_a(0, 2, 2)
+        load_a(1, 0, 2)
+        load_a(1, 2, 2)
+        load_w1(0, 2)
+        load_a(2, 0, 4)
+        load_w1(2, 3)
+
+        ident = keep.tile([P, P], F32)
+        make_identity(nc, ident[:])
+        gate_rows = keep.tile([P, P], F32)
+        nc.gpsimd.memset(gate_rows[:], 0.0)
+        nc.gpsimd.dma_start(out=gate_rows[0:BLOCKS, :], in_=gate[0].rearrange("(b p) -> b p", p=P))
+
+        dc = [keep.tile([P, T], F32, name="dc_%d" % t) for t in range(ROWS)]
+        slope = {key: keep.tile(list(raw.shape), F32, name="slope_%d_%d" % key) for key, raw in a_raw.items()}
+        picked = {key: keep.tile(list(raw.shape), F32, name="picked_%d_%d" % key) for key, raw in a_raw.items()}
+        gate_cols = keep.tile([P, BLOCKS], F32)
+        out_sb = keep.tile([P, T], F32)
+        da_rows = {}
+        da_codes = {}
+        w1_codes = {}
+        dx_sb = {}
+
+        def window(t, vector_cut):
+            for c, (lo, hi) in enumerate(TOKEN_CUTS):
+                bank = psum.tile([P, hi - lo], F32, name="wide", tag="wide", bufs=5)
+                nc.tensor.matmul_mx(
+                    out=bank[:],
+                    lhsT=w2_codes[:, 2 * P * t : 2 * P * (t + 1)].bitcast(FP4X4),
+                    lhsT_scale=w2_plane[:, P * t : P * (t + 1)],
+                    rhs=dy_codes[:, lo:hi].bitcast(FP8X4),
+                    rhs_scale=dy_plane[:, lo:hi],
+                    start=True,
+                    stop=True,
+                )
+                if c == vector_cut:
+                    nc.vector.tensor_copy(out=dc[t][:, lo:hi], in_=bank[:])
+                else:
+                    nc.scalar.copy(out=dc[t][:, lo:hi], in_=bank[:])
+
+        def relu_vector(ci, t):
+            nc.vector.tensor_scalar(out=slope[ci, t][:], in0=a_raw[ci, t], scalar1=0.0, scalar2=2.0, op0=ALU.max, op1=ALU.mult)
+
+        def relu_scalar(ci, t):
+            nc.scalar.activation(out=slope[ci, t][:], in_=a_raw[ci, t], func=ACT.Relu, scale=2.0)
+
+        def gather(ci, t):
+            lo, hi = CHUNKS[ci]
+            nc.vector.tensor_tensor(
+                picked[ci, t][:], dc[t][:].indirect(offsets[:, lo // PER_COL : hi // PER_COL]), slope[ci, t][:], ALU.mult
+            )
+
+        def gate_block(b):
+            ci = max(i for i, cut in enumerate(CHUNKS) if cut[0] <= P * b)
+            first = P * b - CHUNKS[ci][0]
+            turned = psum.tile([P, H], F32, name="wide", tag="wide", bufs=5)
+            for t in range(ROWS):
+                nc.tensor.transpose(turned[:, P * t : P * (t + 1)], picked[ci, t][:, first : first + P], ident[:])
+            da_rows[b] = keep.tile([P, 2, P, 2], BF16, name="da_rows_%d" % b)
+            nc.scalar.activation(
+                out=da_rows[b][:],
+                in_=turned[:].rearrange("s (p u d) -> s u p d", u=2, d=2),
+                func=ACT.Copy,
+                scale=gate_cols[:, b : b + 1],
+            )
+
+        def turn_back(e):
+            back = psum.tile([P, 2, 2, P], F32, name="back", tag="back", bufs=2)
+            for h in range(2):
+                words = da_rows[2 * e + h][:].rearrange("s u p d -> s (u p d)").bitcast(F32)
+                for u in range(2):
+                    nc.tensor.transpose(back[:, h, u, :], words[:, P * u : P * (u + 1)], ident[:])
+            grouped = keep.tile([P, C * PACK], BF16, name="da_grouped_%d" % e, align_bytes=64)
+            nc.scalar.copy(
+                out=grouped[:].bitcast(F32).rearrange("p (h s u) -> p h s u", h=2, u=2),
+                in_=back[:].rearrange("p h u s -> p h s u"),
+            )
+            codes = keep.tile([P, C], U32, name="da_codes_%d" % e, align_bytes=64)
+            plane = keep.tile([P, C], U8, name="da_plane_%d" % e, align_bytes=64)
+            nc.vector.quantize_mx(out=codes[:].bitcast(FP8X4), scales=plane[:], in_=grouped[:])
+            da_codes[e] = (codes, plane)
+
+        def expert_weights(e):
+            grouped = keep.tile([P, K * PACK], BF16, name="w1_grouped_%d" % e, align_bytes=64)
+            nc.scalar.copy(
+                out=grouped[:].rearrange("p (c i j) -> p c j i", i=4, j=PACK),
+                in_=w1_raw[e].rearrange("p j (c i) -> p c j i", i=4),
+            )
+            codes = keep.tile([P, K], U32, name="w1_codes_%d" % e, align_bytes=64)
+            plane = keep.tile([P, K], U8, name="w1_plane_%d" % e, align_bytes=64)
+            nc.vector.quantize_mx(out=codes[:].bitcast(FP8X4), scales=plane[:], in_=grouped[:])
+            w1_codes[e] = (codes, plane)
+
+        def expert_product(e):
+            acc = psum.tile([P, C], F32, name="acc", tag="acc", bufs=1)
+            nc.tensor.matmul_mx(
+                out=acc[:],
+                lhsT=w1_codes[e][0][:].bitcast(FP8X4),
+                lhsT_scale=w1_codes[e][1][:],
+                rhs=da_codes[e][0][:].bitcast(FP8X4),
+                rhs_scale=da_codes[e][1][:],
+                start=True,
+                stop=True,
+            )
+            dx_sb[e] = keep.tile([P, C], F32, name="dx_%d" % e)
+            nc.scalar.copy(out=dx_sb[e][:], in_=acc[:])
+
+        def scatter(e):
+            cols = slice(e * C // PER_COL, (e + 1) * C // PER_COL)
+            nc.vector.tensor_copy(out_sb[:].indirect(offsets[:, cols]), dx_sb[e][:])
+
+        relu_vector(0, 0)
+        relu_vector(0, 1)
+        window(0, 1)
+        gather(0, 0)
+        window(1, None)
+        relu_vector(0, 2)
+        gather(0, 1)
+        window(2, None)
+        relu_vector(0, 3)
+        gather(0, 2)
+        window(3, None)
+        gather(0, 3)
+
+        gate_turned = psum.tile([P, P], F32, name="back", tag="back", bufs=2)
+        nc.tensor.transpose(gate_turned[:], gate_rows[:], ident[:])
+        nc.scalar.copy(out=gate_cols[:], in_=gate_turned[:, 0:BLOCKS])
+
+        for t in range(ROWS):
+            relu_scalar(1, t)
+            gather(1, t)
+        for b in range(4):
+            gate_block(b)
+        for t in range(ROWS):
+            relu_scalar(2, t)
+            gather(2, t)
+        expert_weights(0)
+        turn_back(0)
+        expert_weights(1)
+        turn_back(1)
+        expert_product(0)
+        scatter(0)
+        gate_block(4)
+        gate_block(5)
+        expert_product(1)
+        scatter(1)
+        expert_weights(2)
+        turn_back(2)
+        gate_block(6)
+        gate_block(7)
+        expert_product(2)
+        scatter(2)
+        expert_weights(3)
+        turn_back(3)
+        gate_block(8)
+        gate_block(9)
+        expert_product(3)
+        scatter(3)
+        expert_weights(4)
+        turn_back(4)
+        expert_product(4)
+        scatter(4)
+        nc.sync.dma_start(out=out, in_=out_sb[:])

@@ -40,22 +40,35 @@ def tile_moe_sdb_relu2_kernel(tc, dy_words, dy_scales, w2t_words, w2t_scales, w1
 
         nc.vector.memset(dy_plane[:].bitcast(I32), 0)
         nc.gpsimd.memset(w2_plane[:].bitcast(I32), 0)
+        nc.sync.dma_start(offsets[:], offs)
         nc.sync.dma_start(out=w2_codes[:].bitcast(I32), in_=w2t_words[0].bitcast(I32))
         nc.sync.dma_start(out=dy_codes[:].bitcast(I32), in_=dy_words[0].rearrange("p t d -> p (t d)").bitcast(I32))
         for r in range(4):
             nc.sync.dma_start(out=dy_plane[:].bitcast(I32)[r:P:32, :], in_=dy_scales[0].bitcast(I32)[r:16:4, :])
         for r in range(4):
-            queue = nc.gpsimd if r < 2 else nc.sync
+            queue = nc.gpsimd if r < 1 else nc.sync
             queue.dma_start(out=w2_plane[:].bitcast(I32)[r:P:32, :], in_=w2t_scales[0].bitcast(I32)[r:16:4, :])
 
         a_raw = {}
+        a_pair = {}
+
+        slopes = [keep.tile([P, 2 * 512], F32, name="slope_%d" % h, align_bytes=64) for h in range(2)]
 
         def load_a(ci, t0, count):
             lo, hi = CHUNKS[ci]
-            rows = keep.tile([P, count, hi - lo], F32, name="a_raw_%d_%d" % (ci, t0))
-            nc.sync.dma_start(out=rows[:], in_=a[P * t0 : P * (t0 + count), lo:hi].rearrange("(t p) j -> p t j", p=P))
+            if ci == 0 and t0 >= 2:
+                rows = slopes[0][:, 512 * (t0 - 2) : 512 * (t0 - 1)]
+            else:
+                rows = keep.tile([P, count * (hi - lo)], F32, name="a_raw_%d_%d" % (ci, t0), align_bytes=64)
+            nc.sync.dma_start(
+                out=rows[:].rearrange("p (t j) -> p t j", t=count),
+                in_=a[P * t0 : P * (t0 + count), lo:hi].rearrange("(t p) j -> p t j", p=P),
+            )
             for t in range(count):
-                a_raw[ci, t0 + t] = rows[:, t, :]
+                a_raw[ci, t0 + t] = rows[:, t * (hi - lo) : (t + 1) * (hi - lo)]
+            for h in range(count // 2):
+                a_pair[ci, t0 // 2 + h] = rows[:, 2 * h * (hi - lo) : 2 * (h + 1) * (hi - lo)]
+            return rows
 
         w1_raw = {}
 
@@ -64,24 +77,31 @@ def tile_moe_sdb_relu2_kernel(tc, dy_words, dy_scales, w2t_words, w2t_scales, w1
             nc.sync.dma_start(out=rows[:], in_=w1t[e0 : e0 + count].rearrange("e (p j) k -> p e j k", j=PACK))
             for e in range(count):
                 w1_raw[e0 + e] = rows[:, e, :, :]
+            return rows
 
-        load_a(0, 0, 2)
-        nc.sync.dma_start(offsets[:], offs)
-        load_a(0, 2, 2)
+        for t in range(ROWS):
+            load_a(0, t, 1)
         load_a(1, 0, 2)
-        load_a(1, 2, 2)
+        spent_high = load_a(1, 2, 2)
+        gate_rows = keep.tile([P, P], F32)
+        nc.gpsimd.memset(gate_rows[:], 0.0)
+        nc.sync.dma_start(out=gate_rows[0:BLOCKS, :], in_=gate[0].rearrange("(b p) -> b p", p=P))
         load_w1(0, 2)
         load_a(2, 0, 4)
-        load_w1(2, 3)
+        w1_late = load_w1(2, 3)
 
         ident = keep.tile([P, P], F32)
         make_identity(nc, ident[:])
-        gate_rows = keep.tile([P, P], F32)
-        nc.gpsimd.memset(gate_rows[:], 0.0)
-        nc.gpsimd.dma_start(out=gate_rows[0:BLOCKS, :], in_=gate[0].rearrange("(b p) -> b p", p=P))
 
+        banks = [psum.tile([P, 512], F32, name="bank_%d" % n) for n in range(8)]
         dc = [keep.tile([P, T], F32, name="dc_%d" % t) for t in range(ROWS)]
-        slope = {key: keep.tile(list(raw.shape), F32, name="slope_%d_%d" % key) for key, raw in a_raw.items()}
+        slope = {}
+        for ci, t in a_raw:
+            width = CHUNKS[ci][1] - CHUNKS[ci][0]
+            if ci == 0:
+                slope[ci, t] = slopes[1][:, width * (t % 2) : width * (t % 2 + 1)]
+            else:
+                slope[ci, t] = slopes[t // 2][:, width * (t % 2) : width * (t % 2 + 1)]
         picked = {key: keep.tile(list(raw.shape), F32, name="picked_%d_%d" % key) for key, raw in a_raw.items()}
         gate_cols = keep.tile([P, BLOCKS], F32)
         out_sb = keep.tile([P, T], F32)
@@ -92,9 +112,9 @@ def tile_moe_sdb_relu2_kernel(tc, dy_words, dy_scales, w2t_words, w2t_scales, w1
 
         def window(t, vector_cut):
             for c, (lo, hi) in enumerate(TOKEN_CUTS):
-                bank = psum.tile([P, hi - lo], F32, name="wide", tag="wide", bufs=5)
+                bank = banks[(3 * t + c) % 5][:, 0 : hi - lo]
                 nc.tensor.matmul_mx(
-                    out=bank[:],
+                    out=bank,
                     lhsT=w2_codes[:, 2 * P * t : 2 * P * (t + 1)].bitcast(FP4X4),
                     lhsT_scale=w2_plane[:, P * t : P * (t + 1)],
                     rhs=dy_codes[:, lo:hi].bitcast(FP8X4),
@@ -103,26 +123,27 @@ def tile_moe_sdb_relu2_kernel(tc, dy_words, dy_scales, w2t_words, w2t_scales, w1
                     stop=True,
                 )
                 if c == vector_cut:
-                    nc.vector.tensor_copy(out=dc[t][:, lo:hi], in_=bank[:])
+                    nc.vector.tensor_copy(out=dc[t][:, lo:hi], in_=bank)
                 else:
-                    nc.scalar.copy(out=dc[t][:, lo:hi], in_=bank[:])
+                    nc.scalar.copy(out=dc[t][:, lo:hi], in_=bank)
 
         def relu_vector(ci, t):
-            nc.vector.tensor_scalar(out=slope[ci, t][:], in0=a_raw[ci, t], scalar1=0.0, scalar2=2.0, op0=ALU.max, op1=ALU.mult)
+            nc.vector.tensor_scalar(out=slope[ci, t], in0=a_raw[ci, t], scalar1=0.0, scalar2=2.0, op0=ALU.max, op1=ALU.mult)
 
-        def relu_scalar(ci, t):
-            nc.scalar.activation(out=slope[ci, t][:], in_=a_raw[ci, t], func=ACT.Relu, scale=2.0)
+        def relu_scalar(ci, h):
+            width = 2 * (CHUNKS[ci][1] - CHUNKS[ci][0])
+            nc.scalar.activation(out=slopes[h][:, 0:width], in_=a_pair[ci, h], func=ACT.Relu, scale=2.0)
 
         def gather(ci, t):
             lo, hi = CHUNKS[ci]
             nc.vector.tensor_tensor(
-                picked[ci, t][:], dc[t][:].indirect(offsets[:, lo // PER_COL : hi // PER_COL]), slope[ci, t][:], ALU.mult
+                picked[ci, t][:], dc[t][:].indirect(offsets[:, lo // PER_COL : hi // PER_COL]), slope[ci, t], ALU.mult
             )
 
         def gate_block(b):
             ci = max(i for i, cut in enumerate(CHUNKS) if cut[0] <= P * b)
             first = P * b - CHUNKS[ci][0]
-            turned = psum.tile([P, H], F32, name="wide", tag="wide", bufs=5)
+            turned = banks[5 + b % 2]
             for t in range(ROWS):
                 nc.tensor.transpose(turned[:, P * t : P * (t + 1)], picked[ci, t][:, first : first + P], ident[:])
             da_rows[b] = keep.tile([P, 2, P, 2], BF16, name="da_rows_%d" % b)
@@ -134,7 +155,7 @@ def tile_moe_sdb_relu2_kernel(tc, dy_words, dy_scales, w2t_words, w2t_scales, w1
             )
 
         def turn_back(e):
-            back = psum.tile([P, 2, 2, P], F32, name="back", tag="back", bufs=2)
+            back = banks[e % 2][:].rearrange("p (h u s) -> p h u s", h=2, u=2)
             for h in range(2):
                 words = da_rows[2 * e + h][:].rearrange("s u p d -> s (u p d)").bitcast(F32)
                 for u in range(2):
@@ -142,37 +163,50 @@ def tile_moe_sdb_relu2_kernel(tc, dy_words, dy_scales, w2t_words, w2t_scales, w1
             grouped = keep.tile([P, C * PACK], BF16, name="da_grouped_%d" % e, align_bytes=64)
             nc.scalar.copy(
                 out=grouped[:].bitcast(F32).rearrange("p (h s u) -> p h s u", h=2, u=2),
-                in_=back[:].rearrange("p h u s -> p h s u"),
+                in_=back.rearrange("p h u s -> p h s u"),
             )
             codes = keep.tile([P, C], U32, name="da_codes_%d" % e, align_bytes=64)
             plane = keep.tile([P, C], U8, name="da_plane_%d" % e, align_bytes=64)
             nc.vector.quantize_mx(out=codes[:].bitcast(FP8X4), scales=plane[:], in_=grouped[:])
             da_codes[e] = (codes, plane)
 
-        def expert_weights(e):
-            grouped = keep.tile([P, K * PACK], BF16, name="w1_grouped_%d" % e, align_bytes=64)
+        def quantize_weights(e0, count, grouped):
+            codes = keep.tile([P, count * K], U32, name="w1_codes_%d" % e0, align_bytes=64)
+            plane = keep.tile([P, count * K], U8, name="w1_plane_%d" % e0, align_bytes=64)
+            nc.vector.quantize_mx(out=codes[:].bitcast(FP8X4), scales=plane[:], in_=grouped)
+            for e in range(count):
+                w1_codes[e0 + e] = (codes[:, K * e : K * (e + 1)], plane[:, K * e : K * (e + 1)])
+
+        def early_weights(e):
+            grouped = spent_high[:].bitcast(BF16)[:, K * PACK * e : K * PACK * (e + 1)]
             nc.scalar.copy(
-                out=grouped[:].rearrange("p (c i j) -> p c j i", i=4, j=PACK),
+                out=grouped.rearrange("p (c i j) -> p c j i", i=4, j=PACK),
                 in_=w1_raw[e].rearrange("p j (c i) -> p c j i", i=4),
             )
-            codes = keep.tile([P, K], U32, name="w1_codes_%d" % e, align_bytes=64)
-            plane = keep.tile([P, K], U8, name="w1_plane_%d" % e, align_bytes=64)
-            nc.vector.quantize_mx(out=codes[:].bitcast(FP8X4), scales=plane[:], in_=grouped[:])
-            w1_codes[e] = (codes, plane)
+            quantize_weights(e, 1, grouped)
+
+        def late_weights():
+            grouped = slopes[1][:].bitcast(BF16)[:, 0 : 3 * K * PACK]
+            nc.vector.tensor_copy(
+                out=grouped.rearrange("p (e c i j) -> p c e j i", e=3, i=4, j=PACK),
+                in_=w1_late[:].rearrange("p e j (c i) -> p c e j i", i=4),
+            )
+            quantize_weights(2, 2, grouped[:, 0 : 2 * K * PACK])
+            quantize_weights(4, 1, grouped[:, 2 * K * PACK : 3 * K * PACK])
 
         def expert_product(e):
-            acc = psum.tile([P, C], F32, name="acc", tag="acc", bufs=1)
+            acc = (banks[6] if e == E - 2 else banks[(e + 1) % 2])[:, 0:C]
             nc.tensor.matmul_mx(
-                out=acc[:],
-                lhsT=w1_codes[e][0][:].bitcast(FP8X4),
-                lhsT_scale=w1_codes[e][1][:],
+                out=acc,
+                lhsT=w1_codes[e][0].bitcast(FP8X4),
+                lhsT_scale=w1_codes[e][1],
                 rhs=da_codes[e][0][:].bitcast(FP8X4),
                 rhs_scale=da_codes[e][1][:],
                 start=True,
                 stop=True,
             )
             dx_sb[e] = keep.tile([P, C], F32, name="dx_%d" % e)
-            nc.scalar.copy(out=dx_sb[e][:], in_=acc[:])
+            nc.scalar.copy(out=dx_sb[e][:], in_=acc)
 
         def scatter(e):
             cols = slice(e * C // PER_COL, (e + 1) * C // PER_COL)
@@ -182,51 +216,44 @@ def tile_moe_sdb_relu2_kernel(tc, dy_words, dy_scales, w2t_words, w2t_scales, w1
         relu_vector(0, 1)
         window(0, 1)
         gather(0, 0)
-        window(1, None)
         relu_vector(0, 2)
+        window(1, None)
         gather(0, 1)
-        window(2, None)
         relu_vector(0, 3)
+        window(2, None)
         gather(0, 2)
         window(3, None)
         gather(0, 3)
 
-        gate_turned = psum.tile([P, P], F32, name="back", tag="back", bufs=2)
-        nc.tensor.transpose(gate_turned[:], gate_rows[:], ident[:])
+        gate_turned = banks[2][:, 0:P]
+        nc.tensor.transpose(gate_turned, gate_rows[:], ident[:])
         nc.scalar.copy(out=gate_cols[:], in_=gate_turned[:, 0:BLOCKS])
 
-        for t in range(ROWS):
-            relu_scalar(1, t)
-            gather(1, t)
-        for b in range(4):
-            gate_block(b)
-        for t in range(ROWS):
-            relu_scalar(2, t)
-            gather(2, t)
-        expert_weights(0)
+        def slope_and_gather(ci, h):
+            relu_scalar(ci, h)
+            gather(ci, 2 * h)
+            gather(ci, 2 * h + 1)
+
+        slope_and_gather(1, 0)
+        slope_and_gather(1, 1)
+        gate_block(0)
+        gate_block(1)
+        early_weights(0)
         turn_back(0)
-        expert_weights(1)
+        gate_block(2)
+        slope_and_gather(2, 0)
+        gate_block(3)
+        early_weights(1)
+        slope_and_gather(2, 1)
         turn_back(1)
-        expert_product(0)
-        scatter(0)
-        gate_block(4)
-        gate_block(5)
-        expert_product(1)
-        scatter(1)
-        expert_weights(2)
-        turn_back(2)
-        gate_block(6)
-        gate_block(7)
-        expert_product(2)
-        scatter(2)
-        expert_weights(3)
-        turn_back(3)
-        gate_block(8)
-        gate_block(9)
-        expert_product(3)
-        scatter(3)
-        expert_weights(4)
-        turn_back(4)
-        expert_product(4)
-        scatter(4)
+        late_weights()
+        for e in range(2, E):
+            gate_block(2 * e)
+            expert_product(e - 2)
+            scatter(e - 2)
+            gate_block(2 * e + 1)
+            turn_back(e)
+        for e in range(E - 2, E):
+            expert_product(e)
+            scatter(e)
         nc.sync.dma_start(out=out, in_=out_sb[:])

@@ -1,7 +1,6 @@
 from contextlib import ExitStack
 
 import concourse.mybir as mybir
-from concourse.masks import make_identity
 
 K, T, E, C, H, N = 128, 1280, 5, 256, 512, 512
 FLOPS = 2 * N * H * T + 2 * H * K * E * C
@@ -19,11 +18,8 @@ ALU = mybir.AluOpType
 
 P = 128
 PACK = 4
-ROWS = H // P
-BLOCKS = T // P
 PER_COL = 16
 TOKEN_CUTS = ((0, 512), (512, 1024), (1024, 1280))
-CHUNKS = ((0, 512), (512, 1024), (1024, 1280))
 
 
 def tile_moe_sdb_relu2_kernel(tc, dy_words, dy_scales, w2t_words, w2t_scales, w1t, a, gate, offs, out):
@@ -35,84 +31,78 @@ def tile_moe_sdb_relu2_kernel(tc, dy_words, dy_scales, w2t_words, w2t_scales, w1
         offsets = keep.tile([P, T // PER_COL], U16, name="offsets")
         dy_codes = keep.tile([P, T], U32, align_bytes=64)
         dy_plane = keep.tile([P, T], U8, align_bytes=64)
+        w2_codes_in = keep.tile([P, 2 * H], U8, align_bytes=64)
+        w2_plane_in = keep.tile([P, H], U8, align_bytes=64)
         w2_codes = keep.tile([P, 2 * H], U8, align_bytes=64)
         w2_plane = keep.tile([P, H], U8, align_bytes=64)
 
+        nc.gpsimd.memset(w2_plane_in[:].bitcast(I32), 0)
         nc.vector.memset(dy_plane[:].bitcast(I32), 0)
-        nc.gpsimd.memset(w2_plane[:].bitcast(I32), 0)
-        nc.sync.dma_start(offsets[:], offs)
-        nc.sync.dma_start(out=w2_codes[:].bitcast(I32), in_=w2t_words[0].bitcast(I32))
+        nc.sync.dma_start(out=w2_codes_in[:].bitcast(I32), in_=w2t_words[0].bitcast(I32))
         nc.sync.dma_start(out=dy_codes[:].bitcast(I32), in_=dy_words[0].rearrange("p t d -> p (t d)").bitcast(I32))
         for r in range(4):
-            nc.sync.dma_start(out=dy_plane[:].bitcast(I32)[r:P:32, :], in_=dy_scales[0].bitcast(I32)[r:16:4, :])
+            nc.sync.dma_start(out=w2_plane_in[:].bitcast(I32)[r:P:32, :], in_=w2t_scales[0].bitcast(I32)[r:16:4, :])
         for r in range(4):
             queue = nc.gpsimd if r < 1 else nc.sync
-            queue.dma_start(out=w2_plane[:].bitcast(I32)[r:P:32, :], in_=w2t_scales[0].bitcast(I32)[r:16:4, :])
+            queue.dma_start(out=dy_plane[:].bitcast(I32)[r:P:32, :], in_=dy_scales[0].bitcast(I32)[r:16:4, :])
+        nc.sync.dma_start(offsets[:], offs)
 
-        a_raw = {}
-        a_pair = {}
-
-        slopes = [keep.tile([P, 2 * 512], F32, name="slope_%d" % h, align_bytes=64) for h in range(2)]
-
-        def load_a(ci, t0, count):
-            lo, hi = CHUNKS[ci]
-            if ci == 0 and t0 >= 2:
-                rows = slopes[0][:, 512 * (t0 - 2) : 512 * (t0 - 1)]
-            else:
-                rows = keep.tile([P, count * (hi - lo)], F32, name="a_raw_%d_%d" % (ci, t0), align_bytes=64)
-            nc.sync.dma_start(
-                out=rows[:].rearrange("p (t j) -> p t j", t=count),
-                in_=a[P * t0 : P * (t0 + count), lo:hi].rearrange("(t p) j -> p t j", p=P),
-            )
-            for t in range(count):
-                a_raw[ci, t0 + t] = rows[:, t * (hi - lo) : (t + 1) * (hi - lo)]
-            for h in range(count // 2):
-                a_pair[ci, t0 // 2 + h] = rows[:, 2 * h * (hi - lo) : 2 * (h + 1) * (hi - lo)]
-            return rows
-
+        gate_sb = {}
+        a_sb = {}
         w1_raw = {}
+
+        def load_gate(lo, hi):
+            rows = keep.tile([P, hi - lo], F32, name="gate_%d" % lo)
+            nc.sync.dma_start(out=rows[:], in_=gate[:, lo:hi])
+            for e in range(lo // C, hi // C):
+                gate_sb[e] = rows[:, e * C - lo : (e + 1) * C - lo]
+
+        def load_a(lo, hi):
+            rows = keep.tile([P, PACK, hi - lo], F32, name="a_%d" % lo)
+            nc.sync.dma_start(out=rows[:], in_=a[:, lo:hi].rearrange("(p t) j -> p t j", t=PACK))
+            for e in range(lo // C, hi // C):
+                a_sb[e] = rows[:, :, e * C - lo : (e + 1) * C - lo]
 
         def load_w1(e0, count):
             rows = keep.tile([P, count, PACK, K], F32, name="w1_raw_%d" % e0)
             nc.sync.dma_start(out=rows[:], in_=w1t[e0 : e0 + count].rearrange("e (p j) k -> p e j k", j=PACK))
             for e in range(count):
                 w1_raw[e0 + e] = rows[:, e, :, :]
-            return rows
 
-        for t in range(ROWS):
-            load_a(0, t, 1)
-        load_a(1, 0, 2)
-        spent_high = load_a(1, 2, 2)
-        gate_rows = keep.tile([P, P], F32)
-        nc.gpsimd.memset(gate_rows[:], 0.0)
-        nc.sync.dma_start(out=gate_rows[0:BLOCKS, :], in_=gate[0].rearrange("(b p) -> b p", p=P))
         load_w1(0, 2)
-        load_a(2, 0, 4)
-        w1_late = load_w1(2, 3)
+        load_gate(0, 512)
+        load_gate(512, T)
+        load_a(0, 512)
+        load_w1(2, 3)
+        load_a(512, 1024)
+        load_a(1024, T)
 
-        ident = keep.tile([P, P], F32)
-        make_identity(nc, ident[:])
+        nc.vector.tensor_copy(
+            out=w2_codes[:].bitcast(U16).rearrange("p (t m) -> p t m", t=PACK),
+            in_=w2_codes_in[:].bitcast(U16).rearrange("p (m t) -> p t m", t=PACK),
+        )
+        nc.vector.tensor_copy(
+            out=w2_plane[:].rearrange("p (t m) -> p t m", t=PACK),
+            in_=w2_plane_in[:].rearrange("p (m t) -> p t m", t=PACK),
+        )
 
         banks = [psum.tile([P, 512], F32, name="bank_%d" % n) for n in range(8)]
-        dc = [keep.tile([P, T], F32, name="dc_%d" % t) for t in range(ROWS)]
-        slope = {}
-        for ci, t in a_raw:
-            width = CHUNKS[ci][1] - CHUNKS[ci][0]
-            if ci == 0:
-                slope[ci, t] = slopes[1][:, width * (t % 2) : width * (t % 2 + 1)]
-            else:
-                slope[ci, t] = slopes[t // 2][:, width * (t % 2) : width * (t % 2 + 1)]
-        picked = {key: keep.tile(list(raw.shape), F32, name="picked_%d_%d" % key) for key, raw in a_raw.items()}
-        gate_cols = keep.tile([P, BLOCKS], F32)
+        dc = [keep.tile([P, T], F32, name="dc_%d" % t) for t in range(PACK)]
         out_sb = keep.tile([P, T], F32)
-        da_rows = {}
+        gated = {}
+        for first in range(2):
+            users = range(first, E, 2)
+            rows = keep.tile([P, len(users) + PACK - 1, C], F32, name="gated_%d" % first)
+            for n, e in enumerate(reversed(users)):
+                gated[e] = rows[:, n : n + PACK, :]
+        grouped = {}
         da_codes = {}
         w1_codes = {}
         dx_sb = {}
 
-        def window(t, vector_cut):
+        def window(t):
             for c, (lo, hi) in enumerate(TOKEN_CUTS):
-                bank = banks[(3 * t + c) % 5][:, 0 : hi - lo]
+                bank = banks[(3 * t + c) % 6][:, 0 : hi - lo]
                 nc.tensor.matmul_mx(
                     out=bank,
                     lhsT=w2_codes[:, 2 * P * t : 2 * P * (t + 1)].bitcast(FP4X4),
@@ -122,84 +112,50 @@ def tile_moe_sdb_relu2_kernel(tc, dy_words, dy_scales, w2t_words, w2t_scales, w1
                     start=True,
                     stop=True,
                 )
-                if c == vector_cut:
-                    nc.vector.tensor_copy(out=dc[t][:, lo:hi], in_=bank)
-                else:
-                    nc.scalar.copy(out=dc[t][:, lo:hi], in_=bank)
+                nc.scalar.activation(out=dc[t][:, lo:hi], in_=bank, func=ACT.Copy, scale=2.0)
 
-        def relu_vector(ci, t):
-            nc.vector.tensor_scalar(out=slope[ci, t], in0=a_raw[ci, t], scalar1=0.0, scalar2=2.0, op0=ALU.max, op1=ALU.mult)
+        def gather(e, t):
+            cols = slice(e * C // PER_COL, (e + 1) * C // PER_COL)
+            nc.vector.tensor_tensor(gated[e][:, t, :], dc[t][:].indirect(offsets[:, cols]), gate_sb[e], ALU.mult)
 
-        def relu_scalar(ci, h):
-            width = 2 * (CHUNKS[ci][1] - CHUNKS[ci][0])
-            nc.scalar.activation(out=slopes[h][:, 0:width], in_=a_pair[ci, h], func=ACT.Relu, scale=2.0)
-
-        def gather(ci, t):
-            lo, hi = CHUNKS[ci]
-            nc.vector.tensor_tensor(
-                picked[ci, t][:], dc[t][:].indirect(offsets[:, lo // PER_COL : hi // PER_COL]), slope[ci, t], ALU.mult
+        def slope(e):
+            grouped[e] = keep.tile([P, C * PACK], BF16, name="da_grouped_%d" % e, align_bytes=64)
+            nc.vector.scalar_tensor_tensor(
+                out=grouped[e][:].rearrange("p (s t) -> p s t", t=PACK),
+                in0=a_sb[e].rearrange("p t s -> p s t"),
+                scalar=0.0,
+                in1=gated[e].rearrange("p t s -> p s t"),
+                op0=ALU.max,
+                op1=ALU.mult,
             )
 
-        def gate_block(b):
-            ci = max(i for i, cut in enumerate(CHUNKS) if cut[0] <= P * b)
-            first = P * b - CHUNKS[ci][0]
-            turned = banks[5 + b % 2]
-            for t in range(ROWS):
-                nc.tensor.transpose(turned[:, P * t : P * (t + 1)], picked[ci, t][:, first : first + P], ident[:])
-            da_rows[b] = keep.tile([P, 2, P, 2], BF16, name="da_rows_%d" % b)
-            nc.scalar.activation(
-                out=da_rows[b][:],
-                in_=turned[:].rearrange("s (p u d) -> s u p d", u=2, d=2),
-                func=ACT.Copy,
-                scale=gate_cols[:, b : b + 1],
-            )
-
-        def turn_back(e):
-            back = banks[e % 2][:].rearrange("p (h u s) -> p h u s", h=2, u=2)
-            for h in range(2):
-                words = da_rows[2 * e + h][:].rearrange("s u p d -> s (u p d)").bitcast(F32)
-                for u in range(2):
-                    nc.tensor.transpose(back[:, h, u, :], words[:, P * u : P * (u + 1)], ident[:])
-            grouped = keep.tile([P, C * PACK], BF16, name="da_grouped_%d" % e, align_bytes=64)
-            nc.scalar.copy(
-                out=grouped[:].bitcast(F32).rearrange("p (h s u) -> p h s u", h=2, u=2),
-                in_=back.rearrange("p h u s -> p h s u"),
-            )
+        def quantize_da(e):
             codes = keep.tile([P, C], U32, name="da_codes_%d" % e, align_bytes=64)
             plane = keep.tile([P, C], U8, name="da_plane_%d" % e, align_bytes=64)
-            nc.vector.quantize_mx(out=codes[:].bitcast(FP8X4), scales=plane[:], in_=grouped[:])
+            nc.vector.quantize_mx(out=codes[:].bitcast(FP8X4), scales=plane[:], in_=grouped[e][:])
             da_codes[e] = (codes, plane)
 
-        def quantize_weights(e0, count, grouped):
-            codes = keep.tile([P, count * K], U32, name="w1_codes_%d" % e0, align_bytes=64)
-            plane = keep.tile([P, count * K], U8, name="w1_plane_%d" % e0, align_bytes=64)
-            nc.vector.quantize_mx(out=codes[:].bitcast(FP8X4), scales=plane[:], in_=grouped)
-            for e in range(count):
-                w1_codes[e0 + e] = (codes[:, K * e : K * (e + 1)], plane[:, K * e : K * (e + 1)])
+        w1_grouped = {}
 
-        def early_weights(e):
-            grouped = spent_high[:].bitcast(BF16)[:, K * PACK * e : K * PACK * (e + 1)]
-            nc.scalar.copy(
-                out=grouped.rearrange("p (c i j) -> p c j i", i=4, j=PACK),
+        def round_weights(e, engine_copy):
+            w1_grouped[e] = keep.tile([P, K * PACK], BF16, name="w1_grouped_%d" % e, align_bytes=64)
+            engine_copy(
+                out=w1_grouped[e][:].rearrange("p (c i j) -> p c j i", i=4, j=PACK),
                 in_=w1_raw[e].rearrange("p j (c i) -> p c j i", i=4),
             )
-            quantize_weights(e, 1, grouped)
 
-        def late_weights():
-            grouped = slopes[1][:].bitcast(BF16)[:, 0 : 3 * K * PACK]
-            nc.vector.tensor_copy(
-                out=grouped.rearrange("p (e c i j) -> p c e j i", e=3, i=4, j=PACK),
-                in_=w1_late[:].rearrange("p e j (c i) -> p c e j i", i=4),
-            )
-            quantize_weights(2, 2, grouped[:, 0 : 2 * K * PACK])
-            quantize_weights(4, 1, grouped[:, 2 * K * PACK : 3 * K * PACK])
+        def quantize_weights(e):
+            codes = keep.tile([P, K], U32, name="w1_codes_%d" % e, align_bytes=64)
+            plane = keep.tile([P, K], U8, name="w1_plane_%d" % e, align_bytes=64)
+            nc.vector.quantize_mx(out=codes[:].bitcast(FP8X4), scales=plane[:], in_=w1_grouped[e][:])
+            w1_codes[e] = (codes, plane)
 
         def expert_product(e):
-            acc = (banks[6] if e == E - 2 else banks[(e + 1) % 2])[:, 0:C]
+            acc = banks[6 + e % 2][:, 0:C]
             nc.tensor.matmul_mx(
                 out=acc,
-                lhsT=w1_codes[e][0].bitcast(FP8X4),
-                lhsT_scale=w1_codes[e][1],
+                lhsT=w1_codes[e][0][:].bitcast(FP8X4),
+                lhsT_scale=w1_codes[e][1][:],
                 rhs=da_codes[e][0][:].bitcast(FP8X4),
                 rhs_scale=da_codes[e][1][:],
                 start=True,
@@ -210,50 +166,39 @@ def tile_moe_sdb_relu2_kernel(tc, dy_words, dy_scales, w2t_words, w2t_scales, w1
 
         def scatter(e):
             cols = slice(e * C // PER_COL, (e + 1) * C // PER_COL)
-            nc.vector.tensor_copy(out_sb[:].indirect(offsets[:, cols]), dx_sb[e][:])
+            nc.scalar.activation(out_sb[:].indirect(offsets[:, cols]), dx_sb[e][:], ACT.Copy)
 
-        relu_vector(0, 0)
-        relu_vector(0, 1)
-        window(0, 1)
-        gather(0, 0)
-        relu_vector(0, 2)
-        window(1, None)
+        window(0)
+        round_weights(0, nc.vector.tensor_copy)
+        round_weights(1, nc.vector.tensor_copy)
+        quantize_weights(0)
+        quantize_weights(1)
+        for e in range(E):
+            gather(e, 0)
+        for t in range(1, PACK):
+            window(t)
         gather(0, 1)
-        relu_vector(0, 3)
-        window(2, None)
         gather(0, 2)
-        window(3, None)
+        gather(1, 1)
         gather(0, 3)
-
-        gate_turned = banks[2][:, 0:P]
-        nc.tensor.transpose(gate_turned, gate_rows[:], ident[:])
-        nc.scalar.copy(out=gate_cols[:], in_=gate_turned[:, 0:BLOCKS])
-
-        def slope_and_gather(ci, h):
-            relu_scalar(ci, h)
-            gather(ci, 2 * h)
-            gather(ci, 2 * h + 1)
-
-        slope_and_gather(1, 0)
-        slope_and_gather(1, 1)
-        gate_block(0)
-        gate_block(1)
-        early_weights(0)
-        turn_back(0)
-        gate_block(2)
-        slope_and_gather(2, 0)
-        gate_block(3)
-        early_weights(1)
-        slope_and_gather(2, 1)
-        turn_back(1)
-        late_weights()
+        gather(1, 2)
+        slope(0)
+        gather(1, 3)
+        quantize_da(0)
+        expert_product(0)
+        scatter(0)
+        slope(1)
         for e in range(2, E):
-            gate_block(2 * e)
-            expert_product(e - 2)
-            scatter(e - 2)
-            gate_block(2 * e + 1)
-            turn_back(e)
-        for e in range(E - 2, E):
-            expert_product(e)
-            scatter(e)
+            round_weights(e, nc.scalar.copy)
+            gather(e, 1)
+            quantize_da(e - 1)
+            expert_product(e - 1)
+            scatter(e - 1)
+            gather(e, 2)
+            gather(e, 3)
+            quantize_weights(e)
+            slope(e)
+        quantize_da(E - 1)
+        expert_product(E - 1)
+        scatter(E - 1)
         nc.sync.dma_start(out=out, in_=out_sb[:])

@@ -29,22 +29,23 @@ def tile_moe_sdb_relu2_kernel(tc, dy_words, dy_scales, w2t_words, w2t_scales, w1
         psum = ctx.enter_context(tc.psum_pool(name="psum", bufs=1))
 
         offsets = keep.tile([P, T // PER_COL], U16, name="offsets")
-        dy_codes = keep.tile([P, T], U32, align_bytes=64)
+        dy_codes = keep.tile([P, T], U32, align_bytes=64, tag="tokens")
         dy_plane = keep.tile([P, T], U8, align_bytes=64)
         w2_codes_in = keep.tile([P, 2 * H], U8, align_bytes=64)
         w2_plane_in = keep.tile([P, H], U8, align_bytes=64)
         w2_codes = keep.tile([P, 2 * H], U8, align_bytes=64)
         w2_plane = keep.tile([P, H], U8, align_bytes=64)
 
-        nc.gpsimd.memset(w2_plane_in[:].bitcast(I32), 0)
+        w2_rows = keep.tile([P, H // 4], I32)
         nc.vector.memset(dy_plane[:].bitcast(I32), 0)
-        nc.sync.dma_start(out=w2_codes_in[:].bitcast(I32), in_=w2t_words[0].bitcast(I32))
-        nc.sync.dma_start(out=dy_codes[:].bitcast(I32), in_=dy_words[0].rearrange("p t d -> p (t d)").bitcast(I32))
+        nc.gpsimd.memset(w2_plane_in[:].bitcast(I32), 0)
         for r in range(4):
-            nc.sync.dma_start(out=w2_plane_in[:].bitcast(I32)[r:P:32, :], in_=w2t_scales[0].bitcast(I32)[r:16:4, :])
+            nc.sync.dma_start(out=w2_rows[r:P:32, :], in_=w2t_scales[0].bitcast(I32)[r:16:4, :])
         for r in range(4):
-            queue = nc.gpsimd if r < 1 else nc.sync
-            queue.dma_start(out=dy_plane[:].bitcast(I32)[r:P:32, :], in_=dy_scales[0].bitcast(I32)[r:16:4, :])
+            if r == 2:
+                nc.sync.dma_start(out=w2_codes_in[:].bitcast(I32), in_=w2t_words[0].bitcast(I32))
+                nc.sync.dma_start(out=dy_codes[:].bitcast(I32), in_=dy_words[0].rearrange("p t d -> p (t d)").bitcast(I32))
+            nc.sync.dma_start(out=dy_plane[:].bitcast(I32)[r:P:32, :], in_=dy_scales[0].bitcast(I32)[r:16:4, :])
         nc.sync.dma_start(offsets[:], offs)
 
         gate_sb = {}
@@ -69,32 +70,34 @@ def tile_moe_sdb_relu2_kernel(tc, dy_words, dy_scales, w2t_words, w2t_scales, w1
             for e in range(count):
                 w1_raw[e0 + e] = rows[:, e, :, :]
 
-        load_w1(0, 2)
-        load_gate(0, 512)
-        load_gate(512, T)
+        load_w1(0, 3)
+        load_gate(0, 768)
         load_a(0, 512)
-        load_w1(2, 3)
-        load_a(512, 1024)
-        load_a(1024, T)
+        load_w1(3, 2)
+        load_gate(768, T)
+        load_a(768, T)
+        load_a(512, 768)
 
-        nc.vector.tensor_copy(
-            out=w2_codes[:].bitcast(U16).rearrange("p (t m) -> p t m", t=PACK),
-            in_=w2_codes_in[:].bitcast(U16).rearrange("p (m t) -> p t m", t=PACK),
-        )
-        nc.vector.tensor_copy(
-            out=w2_plane[:].rearrange("p (t m) -> p t m", t=PACK),
-            in_=w2_plane_in[:].rearrange("p (m t) -> p t m", t=PACK),
-        )
+        for q in range(0, P, 32):
+            nc.vector.tensor_copy(out=w2_plane_in[:].bitcast(I32)[q : q + 4, :], in_=w2_rows[q : q + 4, :])
+        for ts in (slice(0, 1), slice(1, PACK)):
+            nc.vector.tensor_copy(
+                out=w2_codes[:].bitcast(U16).rearrange("p (t m) -> p t m", t=PACK)[:, ts, :],
+                in_=w2_codes_in[:].bitcast(U16).rearrange("p (m t) -> p t m", t=PACK)[:, ts, :],
+            )
+            nc.vector.tensor_copy(
+                out=w2_plane[:].rearrange("p (t m) -> p t m", t=PACK)[:, ts, :],
+                in_=w2_plane_in[:].rearrange("p (m t) -> p t m", t=PACK)[:, ts, :],
+            )
 
         banks = [psum.tile([P, 512], F32, name="bank_%d" % n) for n in range(8)]
         dc = [keep.tile([P, T], F32, name="dc_%d" % t) for t in range(PACK)]
         out_sb = keep.tile([P, T], F32)
-        gated = {}
-        for first in range(2):
-            users = range(first, E, 2)
-            rows = keep.tile([P, len(users) + PACK - 1, C], F32, name="gated_%d" % first)
-            for n, e in enumerate(reversed(users)):
-                gated[e] = rows[:, n : n + PACK, :]
+        gated = {0: keep.tile([P, PACK, C], F32, name="gated_0")[:]}
+        sliding = keep.tile([P, PACK + 1, C], F32)
+        gated[1] = sliding[:, 1 : PACK + 1, :]
+        gated[2] = sliding[:, 0:PACK, :]
+        factor = {3: gated[0], 4: dc[3][:, 0 : PACK * C].rearrange("p (t s) -> p t s", t=PACK)}
         grouped = {}
         da_codes = {}
         w1_codes = {}
@@ -129,6 +132,29 @@ def tile_moe_sdb_relu2_kernel(tc, dy_words, dy_scales, w2t_words, w2t_scales, w1
                 op1=ALU.mult,
             )
 
+        def gather_plain(t):
+            cols = slice(3 * C // PER_COL, T // PER_COL)
+            nc.scalar.activation(picked[:, t, :], dc[t][:].indirect(offsets[:, cols]), ACT.Copy)
+
+        def gated_slope(e):
+            nc.vector.scalar_tensor_tensor(
+                out=factor[e],
+                in0=a_sb[e],
+                scalar=0.0,
+                in1=gate_sb[e].unsqueeze(1).to_broadcast([P, PACK, C]),
+                op0=ALU.max,
+                op1=ALU.mult,
+            )
+
+        def weave_product(e):
+            grouped[e] = keep.tile([P, C * PACK], BF16, name="da_grouped_%d" % e, align_bytes=64)
+            nc.vector.tensor_tensor(
+                out=grouped[e][:].rearrange("p (c i t) -> p c t i", i=2, t=PACK),
+                in0=picked[:, :, (e - 3) * C : (e - 2) * C].rearrange("p t (c i) -> p c t i", i=2),
+                in1=factor[e].rearrange("p t (c i) -> p c t i", i=2),
+                op=ALU.mult,
+            )
+
         def quantize_da(e):
             codes = keep.tile([P, C], U32, name="da_codes_%d" % e, align_bytes=64)
             plane = keep.tile([P, C], U8, name="da_plane_%d" % e, align_bytes=64)
@@ -150,8 +176,8 @@ def tile_moe_sdb_relu2_kernel(tc, dy_words, dy_scales, w2t_words, w2t_scales, w1
             nc.vector.quantize_mx(out=codes[:].bitcast(FP8X4), scales=plane[:], in_=w1_grouped[e][:])
             w1_codes[e] = (codes, plane)
 
-        def expert_product(e):
-            acc = banks[6 + e % 2][:, 0:C]
+        def expert_product(e, engine_copy):
+            acc = banks[6 + len(dx_sb) % 2][:, 0:C]
             nc.tensor.matmul_mx(
                 out=acc,
                 lhsT=w1_codes[e][0][:].bitcast(FP8X4),
@@ -162,43 +188,59 @@ def tile_moe_sdb_relu2_kernel(tc, dy_words, dy_scales, w2t_words, w2t_scales, w1
                 stop=True,
             )
             dx_sb[e] = keep.tile([P, C], F32, name="dx_%d" % e)
-            nc.scalar.copy(out=dx_sb[e][:], in_=acc)
+            engine_copy(out=dx_sb[e][:], in_=acc)
 
         def scatter(e):
             cols = slice(e * C // PER_COL, (e + 1) * C // PER_COL)
             nc.scalar.activation(out_sb[:].indirect(offsets[:, cols]), dx_sb[e][:], ACT.Copy)
 
         window(0)
-        round_weights(0, nc.vector.tensor_copy)
-        round_weights(1, nc.vector.tensor_copy)
-        quantize_weights(0)
-        quantize_weights(1)
-        for e in range(E):
-            gather(e, 0)
+        for e in range(3):
+            round_weights(e, nc.vector.tensor_copy)
+            if e > 0:
+                quantize_weights(e - 1)
+        gather(0, 0)
+        quantize_weights(2)
+        gather(1, 0)
+        gather(2, 0)
         for t in range(1, PACK):
             window(t)
+        picked = keep.tile([P, PACK, 2 * C], F32, align_bytes=64, tag="tokens")
+        for t in range(PACK):
+            gather_plain(t)
         gather(0, 1)
-        gather(0, 2)
         gather(1, 1)
-        gather(0, 3)
+        gather(0, 2)
         gather(1, 2)
-        slope(0)
+        gather(0, 3)
         gather(1, 3)
-        quantize_da(0)
-        expert_product(0)
-        scatter(0)
+        slope(0)
         slope(1)
-        for e in range(2, E):
-            round_weights(e, nc.scalar.copy)
-            gather(e, 1)
-            quantize_da(e - 1)
-            expert_product(e - 1)
-            scatter(e - 1)
-            gather(e, 2)
-            gather(e, 3)
-            quantize_weights(e)
-            slope(e)
-        quantize_da(E - 1)
-        expert_product(E - 1)
-        scatter(E - 1)
+        quantize_da(0)
+        expert_product(0, nc.scalar.copy)
+        round_weights(3, nc.scalar.copy)
+        scatter(0)
+        gated_slope(3)
+        quantize_da(1)
+        expert_product(1, nc.scalar.copy)
+        round_weights(4, nc.scalar.copy)
+        scatter(1)
+        gather(2, 1)
+        weave_product(3)
+        gather(2, 2)
+        quantize_weights(3)
+        gather(2, 3)
+        quantize_da(3)
+        expert_product(3, nc.scalar.copy)
+        scatter(3)
+        slope(2)
+        gated_slope(4)
+        quantize_da(2)
+        expert_product(2, nc.scalar.copy)
+        scatter(2)
+        weave_product(4)
+        quantize_weights(4)
+        quantize_da(4)
+        expert_product(4, nc.vector.tensor_copy)
+        nc.vector.tensor_copy(out_sb[:].indirect(offsets[:, 4 * C // PER_COL : T // PER_COL]), dx_sb[4][:])
         nc.sync.dma_start(out=out, in_=out_sb[:])

@@ -42,7 +42,7 @@ def tile_moe_sdb_relu2_kernel(tc, dy_words, dy_scales, w2t_words, w2t_scales, w1
         for r in range(4):
             nc.sync.dma_start(out=w2_rows[r:P:32, :], in_=w2t_scales[0].bitcast(I32)[r:16:4, :])
         for r in range(4):
-            if r == 2:
+            if r == 0:
                 nc.sync.dma_start(out=w2_codes_in[:].bitcast(I32), in_=w2t_words[0].bitcast(I32))
                 nc.sync.dma_start(out=dy_codes[:].bitcast(I32), in_=dy_words[0].rearrange("p t d -> p (t d)").bitcast(I32))
             nc.sync.dma_start(out=dy_plane[:].bitcast(I32)[r:P:32, :], in_=dy_scales[0].bitcast(I32)[r:16:4, :])
@@ -57,6 +57,7 @@ def tile_moe_sdb_relu2_kernel(tc, dy_words, dy_scales, w2t_words, w2t_scales, w1
             nc.sync.dma_start(out=rows[:], in_=gate[:, lo:hi])
             for e in range(lo // C, hi // C):
                 gate_sb[e] = rows[:, e * C - lo : (e + 1) * C - lo]
+            return rows[:]
 
         def load_a(lo, hi):
             rows = keep.tile([P, PACK, hi - lo], F32, name="a_%d" % lo)
@@ -71,12 +72,12 @@ def tile_moe_sdb_relu2_kernel(tc, dy_words, dy_scales, w2t_words, w2t_scales, w1
                 w1_raw[e0 + e] = rows[:, e, :, :]
 
         load_w1(0, 3)
-        load_gate(0, 768)
+        gate_first = load_gate(0, 768)
         load_a(0, 512)
         load_w1(3, 2)
+        load_a(512, 768)
         load_gate(768, T)
         load_a(768, T)
-        load_a(512, 768)
 
         for q in range(0, P, 32):
             nc.vector.tensor_copy(out=w2_plane_in[:].bitcast(I32)[q : q + 4, :], in_=w2_rows[q : q + 4, :])
@@ -93,11 +94,11 @@ def tile_moe_sdb_relu2_kernel(tc, dy_words, dy_scales, w2t_words, w2t_scales, w1
         banks = [psum.tile([P, 512], F32, name="bank_%d" % n) for n in range(8)]
         dc = [keep.tile([P, T], F32, name="dc_%d" % t) for t in range(PACK)]
         out_sb = keep.tile([P, T], F32)
-        gated = {0: keep.tile([P, PACK, C], F32, name="gated_0")[:]}
-        sliding = keep.tile([P, PACK + 1, C], F32)
-        gated[1] = sliding[:, 1 : PACK + 1, :]
-        gated[2] = sliding[:, 0:PACK, :]
-        factor = {3: gated[0], 4: dc[3][:, 0 : PACK * C].rearrange("p (t s) -> p t s", t=PACK)}
+        gated_rows = keep.tile([P, 11 * C], F32, align_bytes=64)
+        spans = gated_rows[:].rearrange("p (n s) -> p n s", s=C)
+        gated = {0: spans[:, 0:10:3, :], 1: spans[:, 1:11:3, :], 2: spans[:, 2:6, :]}
+        factor = {3: spans[:, 6:10, :], 4: gated[2]}
+        dx_tail = keep.tile([P, 2 * C], F32)
         grouped = {}
         da_codes = {}
         w1_codes = {}
@@ -117,14 +118,18 @@ def tile_moe_sdb_relu2_kernel(tc, dy_words, dy_scales, w2t_words, w2t_scales, w1
                 )
                 nc.scalar.activation(out=dc[t][:, lo:hi], in_=bank, func=ACT.Copy, scale=2.0)
 
-        def gather(e, t):
-            cols = slice(e * C // PER_COL, (e + 1) * C // PER_COL)
-            nc.vector.tensor_tensor(gated[e][:, t, :], dc[t][:].indirect(offsets[:, cols]), gate_sb[e], ALU.mult)
+        def gather(t, lo, hi, span):
+            nc.vector.tensor_tensor(
+                gated_rows[:, span * C : span * C + hi - lo],
+                dc[t][:].indirect(offsets[:, lo // PER_COL : hi // PER_COL]),
+                gate_first[:, lo:hi],
+                ALU.mult,
+            )
 
         def slope(e):
-            grouped[e] = keep.tile([P, C * PACK], BF16, name="da_grouped_%d" % e, align_bytes=64)
+            grouped[e * C] = keep.tile([P, C * PACK], BF16, name="da_grouped_%d" % (e * C), align_bytes=64)
             nc.vector.scalar_tensor_tensor(
-                out=grouped[e][:].rearrange("p (s t) -> p s t", t=PACK),
+                out=grouped[e * C][:].rearrange("p (s t) -> p s t", t=PACK),
                 in0=a_sb[e].rearrange("p t s -> p s t"),
                 scalar=0.0,
                 in1=gated[e].rearrange("p t s -> p s t"),
@@ -136,111 +141,128 @@ def tile_moe_sdb_relu2_kernel(tc, dy_words, dy_scales, w2t_words, w2t_scales, w1
             cols = slice(3 * C // PER_COL, T // PER_COL)
             nc.scalar.activation(picked[:, t, :], dc[t][:].indirect(offsets[:, cols]), ACT.Copy)
 
-        def gated_slope(e):
+        def gated_slope(lo, hi):
+            e, cols = lo // C, slice(lo % C, lo % C + hi - lo)
             nc.vector.scalar_tensor_tensor(
-                out=factor[e],
-                in0=a_sb[e],
+                out=factor[e][:, :, cols],
+                in0=a_sb[e][:, :, cols],
                 scalar=0.0,
-                in1=gate_sb[e].unsqueeze(1).to_broadcast([P, PACK, C]),
+                in1=gate_sb[e][:, cols].unsqueeze(1).to_broadcast([P, PACK, hi - lo]),
                 op0=ALU.max,
                 op1=ALU.mult,
             )
 
-        def weave_product(e):
-            grouped[e] = keep.tile([P, C * PACK], BF16, name="da_grouped_%d" % e, align_bytes=64)
+        def weave_product(lo, hi):
+            first = (lo - 3 * C) % C
+            grouped[lo] = keep.tile([P, (hi - lo) * PACK], BF16, name="da_grouped_%d" % lo, align_bytes=64)
             nc.vector.tensor_tensor(
-                out=grouped[e][:].rearrange("p (c i t) -> p c t i", i=2, t=PACK),
-                in0=picked[:, :, (e - 3) * C : (e - 2) * C].rearrange("p t (c i) -> p c t i", i=2),
-                in1=factor[e].rearrange("p t (c i) -> p c t i", i=2),
+                out=grouped[lo][:].rearrange("p (c i t) -> p c t i", i=2, t=PACK),
+                in0=picked[:, :, lo - 3 * C : hi - 3 * C].rearrange("p t (c i) -> p c t i", i=2),
+                in1=factor[lo // C][:, :, first : first + hi - lo].rearrange("p t (c i) -> p c t i", i=2),
                 op=ALU.mult,
             )
 
-        def quantize_da(e):
-            codes = keep.tile([P, C], U32, name="da_codes_%d" % e, align_bytes=64)
-            plane = keep.tile([P, C], U8, name="da_plane_%d" % e, align_bytes=64)
-            nc.vector.quantize_mx(out=codes[:].bitcast(FP8X4), scales=plane[:], in_=grouped[e][:])
-            da_codes[e] = (codes, plane)
+        def quantize_da(lo, hi):
+            codes = keep.tile([P, hi - lo], U32, name="da_codes_%d" % lo, align_bytes=64)
+            plane = keep.tile([P, hi - lo], U8, name="da_plane_%d" % lo, align_bytes=64)
+            nc.vector.quantize_mx(out=codes[:].bitcast(FP8X4), scales=plane[:], in_=grouped[lo][:])
+            da_codes[lo] = (codes, plane)
 
-        w1_grouped = {}
+        w1_grouped = keep.tile([P, (E - 1) * K * PACK], BF16, align_bytes=64)
+
+        w1_last = []
+
+        def rounded(e0, count):
+            if e0 == E - 1:
+                return w1_last[0][:]
+            return w1_grouped[:, e0 * K * PACK : (e0 + count) * K * PACK]
 
         def round_weights(e, engine_copy):
-            w1_grouped[e] = keep.tile([P, K * PACK], BF16, name="w1_grouped_%d" % e, align_bytes=64)
             engine_copy(
-                out=w1_grouped[e][:].rearrange("p (c i j) -> p c j i", i=4, j=PACK),
+                out=rounded(e, 1).rearrange("p (c i j) -> p c j i", i=4, j=PACK),
                 in_=w1_raw[e].rearrange("p j (c i) -> p c j i", i=4),
             )
 
-        def quantize_weights(e):
-            codes = keep.tile([P, K], U32, name="w1_codes_%d" % e, align_bytes=64)
-            plane = keep.tile([P, K], U8, name="w1_plane_%d" % e, align_bytes=64)
-            nc.vector.quantize_mx(out=codes[:].bitcast(FP8X4), scales=plane[:], in_=w1_grouped[e][:])
-            w1_codes[e] = (codes, plane)
+        def quantize_weights(e0, count):
+            home = e0 if e0 < 3 else e0 - 2
+            codes = keep.tile([P, count * K], U32, name="w1_codes_%d" % home, align_bytes=64)
+            plane = keep.tile([P, count * K], U8, name="w1_plane_%d" % home, align_bytes=64)
+            nc.vector.quantize_mx(
+                out=codes[:].bitcast(FP8X4), scales=plane[:], in_=rounded(e0, count)
+            )
+            for n in range(count):
+                w1_codes[e0 + n] = (codes[:, n * K : (n + 1) * K], plane[:, n * K : (n + 1) * K])
 
-        def expert_product(e, engine_copy):
-            acc = banks[6 + len(dx_sb) % 2][:, 0:C]
+        def expert_product(lo, hi, engine_copy):
+            acc = banks[6 + len(dx_sb) % 2][:, 0 : hi - lo]
             nc.tensor.matmul_mx(
                 out=acc,
-                lhsT=w1_codes[e][0][:].bitcast(FP8X4),
-                lhsT_scale=w1_codes[e][1][:],
-                rhs=da_codes[e][0][:].bitcast(FP8X4),
-                rhs_scale=da_codes[e][1][:],
+                lhsT=w1_codes[lo // C][0].bitcast(FP8X4),
+                lhsT_scale=w1_codes[lo // C][1],
+                rhs=da_codes[lo][0][:].bitcast(FP8X4),
+                rhs_scale=da_codes[lo][1][:],
                 start=True,
                 stop=True,
             )
-            dx_sb[e] = keep.tile([P, C], F32, name="dx_%d" % e)
-            engine_copy(out=dx_sb[e][:], in_=acc)
+            if lo < 3 * C:
+                dx_sb[lo] = keep.tile([P, hi - lo], F32, name="dx_%d" % lo)[:]
+            else:
+                dx_sb[lo] = dx_tail[:, lo - 3 * C : hi - 3 * C]
+            engine_copy(out=dx_sb[lo], in_=acc)
 
-        def scatter(e):
-            cols = slice(e * C // PER_COL, (e + 1) * C // PER_COL)
-            nc.scalar.activation(out_sb[:].indirect(offsets[:, cols]), dx_sb[e][:], ACT.Copy)
+        def scatter(lo, hi):
+            source = dx_sb[lo] if lo < 3 * C else dx_tail[:, lo - 3 * C : hi - 3 * C]
+            nc.scalar.activation(out_sb[:].indirect(offsets[:, lo // PER_COL : hi // PER_COL]), source, ACT.Copy)
 
         window(0)
         for e in range(3):
             round_weights(e, nc.vector.tensor_copy)
             if e > 0:
-                quantize_weights(e - 1)
-        gather(0, 0)
-        quantize_weights(2)
-        gather(1, 0)
-        gather(2, 0)
+                quantize_weights(e - 1, 1)
+        gather(0, 0, 3 * C, 0)
+        quantize_weights(2, 1)
         for t in range(1, PACK):
             window(t)
+            if t < PACK - 1:
+                gather(t, 0, 2 * C, 3 * t)
         picked = keep.tile([P, PACK, 2 * C], F32, align_bytes=64, tag="tokens")
         for t in range(PACK):
             gather_plain(t)
-        gather(0, 1)
-        gather(1, 1)
-        gather(0, 2)
-        gather(1, 2)
-        gather(0, 3)
-        gather(1, 3)
+        gather(3, 0, C, 9)
+        gather(3, C, 2 * C, 10)
         slope(0)
+        gather(3, 2 * C, 3 * C, 5)
+        quantize_da(0, C)
+        expert_product(0, C, nc.scalar.copy)
+        scatter(0, C)
         slope(1)
-        quantize_da(0)
-        expert_product(0, nc.scalar.copy)
+        gather(1, 2 * C, 3 * C, 3)
+        gather(2, 2 * C, 3 * C, 4)
+        quantize_da(C, 2 * C)
+        expert_product(C, 2 * C, nc.scalar.copy)
+        scatter(C, 2 * C)
         round_weights(3, nc.scalar.copy)
-        scatter(0)
-        gated_slope(3)
-        quantize_da(1)
-        expert_product(1, nc.scalar.copy)
-        round_weights(4, nc.scalar.copy)
-        scatter(1)
-        gather(2, 1)
-        weave_product(3)
-        gather(2, 2)
-        quantize_weights(3)
-        gather(2, 3)
-        quantize_da(3)
-        expert_product(3, nc.scalar.copy)
-        scatter(3)
         slope(2)
-        gated_slope(4)
-        quantize_da(2)
-        expert_product(2, nc.scalar.copy)
-        scatter(2)
-        weave_product(4)
-        quantize_weights(4)
-        quantize_da(4)
-        expert_product(4, nc.vector.tensor_copy)
-        nc.vector.tensor_copy(out_sb[:].indirect(offsets[:, 4 * C // PER_COL : T // PER_COL]), dx_sb[4][:])
+        gated_slope(3 * C, 4 * C)
+        quantize_da(2 * C, 3 * C)
+        expert_product(2 * C, 3 * C, nc.scalar.copy)
+        scatter(2 * C, 3 * C)
+        quantize_weights(3, 1)
+        weave_product(3 * C, 4 * C)
+        gated_slope(1024, 1152)
+        quantize_da(3 * C, 4 * C)
+        expert_product(3 * C, 4 * C, nc.scalar.copy)
+        scatter(768, 960)
+        weave_product(1024, 1152)
+        w1_last.append(keep.tile([P, K * PACK], BF16, name="da_grouped_%d" % (2 * C), align_bytes=64))
+        round_weights(4, nc.vector.tensor_copy)
+        quantize_da(1024, 1152)
+        quantize_weights(4, 1)
+        expert_product(1024, 1152, nc.scalar.copy)
+        scatter(960, 1120)
+        gated_slope(1152, T)
+        weave_product(1152, T)
+        quantize_da(1152, T)
+        expert_product(1152, T, nc.vector.tensor_copy)
+        nc.vector.tensor_copy(out_sb[:].indirect(offsets[:, 1120 // PER_COL : T // PER_COL]), dx_tail[:, 1120 - 3 * C : 2 * C])
         nc.sync.dma_start(out=out, in_=out_sb[:])

@@ -19,6 +19,9 @@ ALU = mybir.AluOpType
 P = 128
 PACK = 4
 PER_COL = 16
+ROW_PAD = 10
+WIDE = 3 * C + 6
+NARROW = C + 2
 TOKEN_CUTS = ((0, 512), (512, 1024), (1024, 1280))
 
 
@@ -60,8 +63,9 @@ def tile_moe_sdb_relu2_kernel(tc, dy_words, dy_scales, w2t_words, w2t_scales, w1
             return rows[:]
 
         def load_a(lo, hi):
-            rows = keep.tile([P, PACK, hi - lo], F32, name="a_%d" % lo)
-            nc.sync.dma_start(out=rows[:], in_=a[:, lo:hi].rearrange("(p t) j -> p t j", t=PACK))
+            padded = keep.tile([P, PACK, hi - lo + ROW_PAD], F32, name="a_%d" % lo)
+            rows = padded[:, :, 0 : hi - lo]
+            nc.sync.dma_start(out=rows, in_=a[:, lo:hi].rearrange("(p t) j -> p t j", t=PACK))
             for e in range(lo // C, hi // C):
                 a_sb[e] = rows[:, :, e * C - lo : (e + 1) * C - lo]
 
@@ -94,10 +98,11 @@ def tile_moe_sdb_relu2_kernel(tc, dy_words, dy_scales, w2t_words, w2t_scales, w1
         banks = [psum.tile([P, 512], F32, name="bank_%d" % n) for n in range(8)]
         dc = [keep.tile([P, T], F32, name="dc_%d" % t) for t in range(PACK)]
         out_sb = keep.tile([P, T], F32)
-        gated_rows = keep.tile([P, 11 * C], F32, align_bytes=64)
-        spans = gated_rows[:].rearrange("p (n s) -> p n s", s=C)
-        gated = {0: spans[:, 0:10:3, :], 1: spans[:, 1:11:3, :], 2: spans[:, 2:6, :]}
-        factor = {3: spans[:, 6:10, :], 4: gated[2]}
+        gated_rows = keep.tile([P, PACK * WIDE], F32, align_bytes=64)
+        wide = gated_rows[:].rearrange("p (t s) -> p t s", s=WIDE)
+        narrow = gated_rows[:, 2 * C : 2 * C + PACK * NARROW].rearrange("p (t s) -> p t s", s=NARROW)
+        gated = {0: wide[:, :, 0:C], 1: wide[:, :, C : 2 * C], 2: narrow[:, :, 0:C]}
+        factor = {3: gated_rows[:, 2 * WIDE : 2 * WIDE + PACK * C].rearrange("p (t s) -> p t s", s=C), 4: gated[2]}
         dx_tail = keep.tile([P, 2 * C], F32)
         grouped = {}
         da_codes = {}
@@ -118,9 +123,10 @@ def tile_moe_sdb_relu2_kernel(tc, dy_words, dy_scales, w2t_words, w2t_scales, w1
                 )
                 nc.scalar.activation(out=dc[t][:, lo:hi], in_=bank, func=ACT.Copy, scale=2.0)
 
-        def gather(t, lo, hi, span):
+        def gather(t, lo, hi):
+            first = t * WIDE + lo if lo < 2 * C else t * NARROW + lo
             nc.vector.tensor_tensor(
-                gated_rows[:, span * C : span * C + hi - lo],
+                gated_rows[:, first : first + hi - lo],
                 dc[t][:].indirect(offsets[:, lo // PER_COL : hi // PER_COL]),
                 gate_first[:, lo:hi],
                 ALU.mult,
@@ -219,25 +225,25 @@ def tile_moe_sdb_relu2_kernel(tc, dy_words, dy_scales, w2t_words, w2t_scales, w1
             round_weights(e, nc.vector.tensor_copy)
             if e > 0:
                 quantize_weights(e - 1, 1)
-        gather(0, 0, 3 * C, 0)
+        gather(0, 0, 3 * C)
         quantize_weights(2, 1)
         for t in range(1, PACK):
             window(t)
             if t < PACK - 1:
-                gather(t, 0, 2 * C, 3 * t)
+                gather(t, 0, 2 * C)
         picked = keep.tile([P, PACK, 2 * C], F32, align_bytes=64, tag="tokens")
         for t in range(PACK):
             gather_plain(t)
-        gather(3, 0, C, 9)
-        gather(3, C, 2 * C, 10)
+        gather(3, 0, C)
+        gather(3, C, 2 * C)
         slope(0)
-        gather(3, 2 * C, 3 * C, 5)
+        gather(3, 2 * C, 3 * C)
         quantize_da(0, C)
         expert_product(0, C, nc.scalar.copy)
         scatter(0, C)
         slope(1)
-        gather(1, 2 * C, 3 * C, 3)
-        gather(2, 2 * C, 3 * C, 4)
+        gather(1, 2 * C, 3 * C)
+        gather(2, 2 * C, 3 * C)
         quantize_da(C, 2 * C)
         expert_product(C, 2 * C, nc.scalar.copy)
         scatter(C, 2 * C)

@@ -40,16 +40,19 @@ def tile_moe_sdb_relu2_kernel(tc, dy_words, dy_scales, w2t_words, w2t_scales, w1
         w2_plane = keep.tile([P, H], U8, align_bytes=64)
 
         w2_rows = keep.tile([P, H // 4], I32)
-        nc.vector.memset(dy_plane[:].bitcast(I32), 0)
         nc.gpsimd.memset(w2_plane_in[:].bitcast(I32), 0)
+
+        def load_rows(queue, plane, scales, r):
+            queue.dma_start(out=plane[r:P:32, :], in_=scales[0].bitcast(I32)[r:16:4, :])
+
+        load_rows(nc.sync, w2_rows, w2t_scales, 0)
+        load_rows(nc.scalar, w2_rows, w2t_scales, 1)
+        nc.sync.dma_start(out=w2_codes_in[:].bitcast(I32), in_=w2t_words[0].bitcast(I32))
+        load_rows(nc.scalar, w2_rows, w2t_scales, 2)
+        nc.sync.dma_start(out=dy_codes[:].bitcast(I32), in_=dy_words[0].rearrange("p t d -> p (t d)").bitcast(I32))
+        load_rows(nc.scalar, w2_rows, w2t_scales, 3)
         for r in range(4):
-            nc.sync.dma_start(out=w2_rows[r:P:32, :], in_=w2t_scales[0].bitcast(I32)[r:16:4, :])
-        for r in range(4):
-            if r == 0:
-                nc.sync.dma_start(out=w2_codes_in[:].bitcast(I32), in_=w2t_words[0].bitcast(I32))
-                nc.sync.dma_start(out=dy_codes[:].bitcast(I32), in_=dy_words[0].rearrange("p t d -> p (t d)").bitcast(I32))
-            nc.sync.dma_start(out=dy_plane[:].bitcast(I32)[r:P:32, :], in_=dy_scales[0].bitcast(I32)[r:16:4, :])
-        nc.sync.dma_start(offsets[:], offs)
+            load_rows(nc.scalar if r % 2 else nc.sync, dy_plane[:].bitcast(I32), dy_scales, r)
 
         gate_sb = {}
         a_sb = {}
@@ -75,7 +78,9 @@ def tile_moe_sdb_relu2_kernel(tc, dy_words, dy_scales, w2t_words, w2t_scales, w1
             for e in range(count):
                 w1_raw[e0 + e] = rows[:, e, :, :]
 
-        load_w1(0, 3)
+        load_w1(0, 1)
+        load_w1(1, 2)
+        nc.sync.dma_start(offsets[:], offs)
         gate_first = load_gate(0, 768)
         load_a(0, 512)
         load_w1(3, 2)

@@ -19,10 +19,12 @@ ALU = mybir.AluOpType
 P = 128
 PACK = 4
 PER_COL = 16
+HALF = C // 2
 ROW_PAD = 10
-WIDE = 3 * C + 6
-NARROW = C + 2
-TOKEN_CUTS = ((0, 512), (512, 1024), (1024, 1280))
+EARLY = 2 * C + HALF
+PITCH = EARLY + 6
+FIRST_TOKENS = 768
+TOKEN_CUTS = ((0, 512), (512, FIRST_TOKENS), (FIRST_TOKENS, T))
 
 
 def tile_moe_sdb_relu2_kernel(tc, dy_words, dy_scales, w2t_words, w2t_scales, w1t, a, gate, offs, out):
@@ -38,39 +40,31 @@ def tile_moe_sdb_relu2_kernel(tc, dy_words, dy_scales, w2t_words, w2t_scales, w1
         w2_plane_in = keep.tile([P, H], U8, align_bytes=64)
         w2_codes = keep.tile([P, 2 * H], U8, align_bytes=64)
         w2_plane = keep.tile([P, H], U8, align_bytes=64)
-
         w2_rows = keep.tile([P, H // 4], I32)
-        nc.gpsimd.memset(w2_plane_in[:].bitcast(I32), 0)
-
-        def load_rows(queue, plane, scales, r):
-            queue.dma_start(out=plane[r:P:32, :], in_=scales[0].bitcast(I32)[r:16:4, :])
-
-        load_rows(nc.sync, w2_rows, w2t_scales, 0)
-        load_rows(nc.scalar, w2_rows, w2t_scales, 1)
-        nc.sync.dma_start(out=w2_codes_in[:].bitcast(I32), in_=w2t_words[0].bitcast(I32))
-        load_rows(nc.scalar, w2_rows, w2t_scales, 2)
-        nc.sync.dma_start(out=dy_codes[:].bitcast(I32), in_=dy_words[0].rearrange("p t d -> p (t d)").bitcast(I32))
-        load_rows(nc.scalar, w2_rows, w2t_scales, 3)
-        for r in range(4):
-            load_rows(nc.scalar if r % 2 else nc.sync, dy_plane[:].bitcast(I32), dy_scales, r)
-
         gate_sb = {}
         a_sb = {}
         w1_raw = {}
 
+        def load_scale_rows(plane, scales):
+            for r in range(4):
+                nc.sync.dma_start(out=plane[r:P:32, :], in_=scales[0].bitcast(I32)[r:16:4, :])
+
+        def load_tokens(lo, hi):
+            words = dy_words[0].rearrange("p t d -> p (t d)").bitcast(I32)
+            nc.sync.dma_start(out=dy_codes[:, lo:hi].bitcast(I32), in_=words[:, lo:hi])
+
         def load_gate(lo, hi):
             rows = keep.tile([P, hi - lo], F32, name="gate_%d" % lo)
             nc.sync.dma_start(out=rows[:], in_=gate[:, lo:hi])
-            for e in range(lo // C, hi // C):
-                gate_sb[e] = rows[:, e * C - lo : (e + 1) * C - lo]
-            return rows[:]
+            for first in range(lo, hi, HALF):
+                gate_sb[first] = rows[:, first - lo :]
 
         def load_a(lo, hi):
             padded = keep.tile([P, PACK, hi - lo + ROW_PAD], F32, name="a_%d" % lo)
             rows = padded[:, :, 0 : hi - lo]
             nc.sync.dma_start(out=rows, in_=a[:, lo:hi].rearrange("(p t) j -> p t j", t=PACK))
-            for e in range(lo // C, hi // C):
-                a_sb[e] = rows[:, :, e * C - lo : (e + 1) * C - lo]
+            for first in range(lo, hi, HALF):
+                a_sb[first] = rows[:, :, first - lo :]
 
         def load_w1(e0, count):
             rows = keep.tile([P, count, PACK, K], F32, name="w1_raw_%d" % e0)
@@ -78,15 +72,21 @@ def tile_moe_sdb_relu2_kernel(tc, dy_words, dy_scales, w2t_words, w2t_scales, w1
             for e in range(count):
                 w1_raw[e0 + e] = rows[:, e, :, :]
 
+        nc.gpsimd.memset(w2_plane_in[:].bitcast(I32), 0)
+        load_scale_rows(w2_rows, w2t_scales)
+        nc.sync.dma_start(out=w2_codes_in[:].bitcast(I32), in_=w2t_words[0].bitcast(I32))
+        load_tokens(0, FIRST_TOKENS)
+        load_scale_rows(dy_plane[:].bitcast(I32), dy_scales)
+        load_tokens(FIRST_TOKENS, T)
         load_w1(0, 1)
-        load_w1(1, 2)
+        load_w1(1, 1)
+        load_gate(0, EARLY)
         nc.sync.dma_start(offsets[:], offs)
-        gate_first = load_gate(0, 768)
-        load_a(0, 512)
-        load_w1(3, 2)
-        load_a(512, 768)
-        load_gate(768, T)
-        load_a(768, T)
+        load_a(0, 2 * C)
+        load_w1(2, 3)
+        load_gate(EARLY, T)
+        load_a(3 * C, T)
+        load_a(2 * C, 3 * C)
 
         for q in range(0, P, 32):
             nc.vector.tensor_copy(out=w2_plane_in[:].bitcast(I32)[q : q + 4, :], in_=w2_rows[q : q + 4, :])
@@ -103,16 +103,14 @@ def tile_moe_sdb_relu2_kernel(tc, dy_words, dy_scales, w2t_words, w2t_scales, w1
         banks = [psum.tile([P, 512], F32, name="bank_%d" % n) for n in range(8)]
         dc = [keep.tile([P, T], F32, name="dc_%d" % t) for t in range(PACK)]
         out_sb = keep.tile([P, T], F32)
-        gated_rows = keep.tile([P, PACK * WIDE], F32, align_bytes=64)
-        wide = gated_rows[:].rearrange("p (t s) -> p t s", s=WIDE)
-        narrow = gated_rows[:, 2 * C : 2 * C + PACK * NARROW].rearrange("p (t s) -> p t s", s=NARROW)
-        gated = {0: wide[:, :, 0:C], 1: wide[:, :, C : 2 * C], 2: narrow[:, :, 0:C]}
-        factor = {3: gated_rows[:, 2 * WIDE : 2 * WIDE + PACK * C].rearrange("p (t s) -> p t s", s=C), 4: gated[2]}
-        dx_tail = keep.tile([P, 2 * C], F32)
+        dx = keep.tile([P, T], F32)
+        work = keep.tile([P, PACK, PITCH], F32, align_bytes=64)
+        factor = keep.tile([P, PACK, C], F32, align_bytes=64)
         grouped = {}
         da_codes = {}
+        w1_rounded = {}
         w1_codes = {}
-        dx_sb = {}
+        products = []
 
         def window(t):
             for c, (lo, hi) in enumerate(TOKEN_CUTS):
@@ -128,152 +126,148 @@ def tile_moe_sdb_relu2_kernel(tc, dy_words, dy_scales, w2t_words, w2t_scales, w1
                 )
                 nc.scalar.activation(out=dc[t][:, lo:hi], in_=bank, func=ACT.Copy, scale=2.0)
 
-        def gather(t, lo, hi):
-            first = t * WIDE + lo if lo < 2 * C else t * NARROW + lo
-            nc.vector.tensor_tensor(
-                gated_rows[:, first : first + hi - lo],
-                dc[t][:].indirect(offsets[:, lo // PER_COL : hi // PER_COL]),
-                gate_first[:, lo:hi],
-                ALU.mult,
-            )
+        def slots(lo, hi):
+            return offsets[:, lo // PER_COL : hi // PER_COL]
 
-        def slope(e):
-            grouped[e * C] = keep.tile([P, C * PACK], BF16, name="da_grouped_%d" % (e * C), align_bytes=64)
+        def gated_rows(lo, hi):
+            base = 0 if lo < EARLY else EARLY
+            return work[:, :, lo - base : hi - base]
+
+        def da_values(lo, hi):
+            e = lo // C
+            if e not in grouped:
+                grouped[e] = keep.tile([P, C * PACK], BF16, name="da_values_%d" % e, align_bytes=64)
+            return grouped[e][:, (lo - e * C) * PACK : (hi - e * C) * PACK]
+
+        def gather_gated(t, lo, hi):
+            nc.vector.tensor_tensor(gated_rows(lo, hi)[:, t, :], dc[t][:].indirect(slots(lo, hi)), gate_sb[lo][:, 0 : hi - lo], ALU.mult)
+
+        def slope_product(lo, hi):
             nc.vector.scalar_tensor_tensor(
-                out=grouped[e * C][:].rearrange("p (s t) -> p s t", t=PACK),
-                in0=a_sb[e].rearrange("p t s -> p s t"),
+                out=da_values(lo, hi).rearrange("p (s t) -> p s t", t=PACK),
+                in0=a_sb[lo][:, :, 0 : hi - lo].rearrange("p t s -> p s t"),
                 scalar=0.0,
-                in1=gated[e].rearrange("p t s -> p s t"),
+                in1=gated_rows(lo, hi).rearrange("p t s -> p s t"),
                 op0=ALU.max,
                 op1=ALU.mult,
             )
 
-        def gather_plain(t):
-            cols = slice(3 * C // PER_COL, T // PER_COL)
-            nc.scalar.activation(picked[:, t, :], dc[t][:].indirect(offsets[:, cols]), ACT.Copy)
+        def gather_plain(t, lo, hi):
+            nc.scalar.activation(picked[:, t, lo - 3 * C : hi - 3 * C], dc[t][:].indirect(slots(lo, hi)), ACT.Copy)
 
         def gated_slope(lo, hi):
-            e, cols = lo // C, slice(lo % C, lo % C + hi - lo)
             nc.vector.scalar_tensor_tensor(
-                out=factor[e][:, :, cols],
-                in0=a_sb[e][:, :, cols],
+                out=factor[:, :, lo % C : lo % C + hi - lo],
+                in0=a_sb[lo][:, :, 0 : hi - lo],
                 scalar=0.0,
-                in1=gate_sb[e][:, cols].unsqueeze(1).to_broadcast([P, PACK, hi - lo]),
+                in1=gate_sb[lo][:, 0 : hi - lo].unsqueeze(1).to_broadcast([P, PACK, hi - lo]),
                 op0=ALU.max,
                 op1=ALU.mult,
             )
 
         def weave_product(lo, hi):
-            first = (lo - 3 * C) % C
-            grouped[lo] = keep.tile([P, (hi - lo) * PACK], BF16, name="da_grouped_%d" % lo, align_bytes=64)
             nc.vector.tensor_tensor(
-                out=grouped[lo][:].rearrange("p (c i t) -> p c t i", i=2, t=PACK),
+                out=da_values(lo, hi).rearrange("p (c i t) -> p c t i", i=2, t=PACK),
                 in0=picked[:, :, lo - 3 * C : hi - 3 * C].rearrange("p t (c i) -> p c t i", i=2),
-                in1=factor[lo // C][:, :, first : first + hi - lo].rearrange("p t (c i) -> p c t i", i=2),
+                in1=factor[:, :, lo % C : lo % C + hi - lo].rearrange("p t (c i) -> p c t i", i=2),
                 op=ALU.mult,
             )
 
         def quantize_da(lo, hi):
             codes = keep.tile([P, hi - lo], U32, name="da_codes_%d" % lo, align_bytes=64)
             plane = keep.tile([P, hi - lo], U8, name="da_plane_%d" % lo, align_bytes=64)
-            nc.vector.quantize_mx(out=codes[:].bitcast(FP8X4), scales=plane[:], in_=grouped[lo][:])
+            nc.vector.quantize_mx(out=codes[:].bitcast(FP8X4), scales=plane[:], in_=da_values(lo, hi))
             da_codes[lo] = (codes, plane)
 
-        w1_grouped = keep.tile([P, (E - 1) * K * PACK], BF16, align_bytes=64)
-
-        w1_last = []
-
-        def rounded(e0, count):
-            if e0 == E - 1:
-                return w1_last[0][:]
-            return w1_grouped[:, e0 * K * PACK : (e0 + count) * K * PACK]
-
-        def round_weights(e, engine_copy):
+        def round_weights(e, lo, hi, engine_copy, home):
+            rounded = keep.tile([P, (hi - lo) * PACK], BF16, name=home, align_bytes=64)
             engine_copy(
-                out=rounded(e, 1).rearrange("p (c i j) -> p c j i", i=4, j=PACK),
-                in_=w1_raw[e].rearrange("p j (c i) -> p c j i", i=4),
+                out=rounded[:].rearrange("p (c i j) -> p c j i", i=4, j=PACK),
+                in_=w1_raw[e][:, :, lo:hi].rearrange("p j (c i) -> p c j i", i=4),
             )
+            w1_rounded[e, lo] = rounded
 
-        def quantize_weights(e0, count):
-            home = e0 if e0 < 3 else e0 - 2
-            codes = keep.tile([P, count * K], U32, name="w1_codes_%d" % home, align_bytes=64)
-            plane = keep.tile([P, count * K], U8, name="w1_plane_%d" % home, align_bytes=64)
-            nc.vector.quantize_mx(
-                out=codes[:].bitcast(FP8X4), scales=plane[:], in_=rounded(e0, count)
-            )
-            for n in range(count):
-                w1_codes[e0 + n] = (codes[:, n * K : (n + 1) * K], plane[:, n * K : (n + 1) * K])
+        def quantize_weights(e, lo, hi):
+            if e not in w1_codes:
+                codes = keep.tile([P, K], U32, name="w1_codes_%d" % e, align_bytes=64)
+                plane = keep.tile([P, K], U8, name="w1_plane_%d" % e, align_bytes=64)
+                w1_codes[e] = (codes, plane)
+            codes, plane = w1_codes[e]
+            nc.vector.quantize_mx(out=codes[:, lo:hi].bitcast(FP8X4), scales=plane[:, lo:hi], in_=w1_rounded[e, lo][:])
 
         def expert_product(lo, hi, engine_copy):
-            acc = banks[6 + len(dx_sb) % 2][:, 0 : hi - lo]
+            acc = banks[6 + len(products) % 2][:, 0 : hi - lo]
+            products.append(lo)
             nc.tensor.matmul_mx(
                 out=acc,
-                lhsT=w1_codes[lo // C][0].bitcast(FP8X4),
-                lhsT_scale=w1_codes[lo // C][1],
+                lhsT=w1_codes[lo // C][0][:].bitcast(FP8X4),
+                lhsT_scale=w1_codes[lo // C][1][:],
                 rhs=da_codes[lo][0][:].bitcast(FP8X4),
                 rhs_scale=da_codes[lo][1][:],
                 start=True,
                 stop=True,
             )
-            if lo < 3 * C:
-                dx_sb[lo] = keep.tile([P, hi - lo], F32, name="dx_%d" % lo)[:]
-            else:
-                dx_sb[lo] = dx_tail[:, lo - 3 * C : hi - 3 * C]
-            engine_copy(out=dx_sb[lo], in_=acc)
+            engine_copy(out=dx[:, lo:hi], in_=acc)
 
         def scatter(lo, hi):
-            source = dx_sb[lo] if lo < 3 * C else dx_tail[:, lo - 3 * C : hi - 3 * C]
-            nc.scalar.activation(out_sb[:].indirect(offsets[:, lo // PER_COL : hi // PER_COL]), source, ACT.Copy)
+            nc.scalar.activation(out_sb[:].indirect(slots(lo, hi)), dx[:, lo:hi], ACT.Copy)
+
+        def finish(e, lo, hi, late):
+            expert_product(e * C, (e + 1) * C, nc.scalar.copy)
+            for args in late:
+                round_weights(*args, nc.scalar.copy, "da_codes_%d" % (e * C))
+            scatter(lo, hi)
 
         window(0)
-        for e in range(3):
-            round_weights(e, nc.vector.tensor_copy)
-            if e > 0:
-                quantize_weights(e - 1, 1)
-        gather(0, 0, 3 * C)
-        quantize_weights(2, 1)
-        for t in range(1, PACK):
-            window(t)
-            if t < PACK - 1:
-                gather(t, 0, 2 * C)
+        for e in range(2):
+            round_weights(e, 0, K, nc.vector.tensor_copy, "w1_rounded_%d" % e)
+        for e in range(2):
+            quantize_weights(e, 0, K)
+        gather_gated(0, 0, EARLY)
+        window(1)
+        gather_gated(1, 0, EARLY)
+        window(2)
+        gather_gated(2, 0, EARLY)
+        window(3)
         picked = keep.tile([P, PACK, 2 * C], F32, align_bytes=64, tag="tokens")
         for t in range(PACK):
-            gather_plain(t)
-        gather(3, 0, C)
-        gather(3, C, 2 * C)
-        slope(0)
-        gather(3, 2 * C, 3 * C)
+            gather_plain(t, 3 * C, T)
+        gather_gated(3, 0, C)
+        gather_gated(3, C, 2 * C)
+        slope_product(0, C)
+        gated_slope(768, 896)
         quantize_da(0, C)
-        expert_product(0, C, nc.scalar.copy)
-        scatter(0, C)
-        slope(1)
-        gather(1, 2 * C, 3 * C)
-        gather(2, 2 * C, 3 * C)
+        finish(0, 0, C, [(4, 0, K)])
+        slope_product(C, 2 * C)
+        round_weights(3, 0, K, nc.vector.tensor_copy, "da_values_0")
         quantize_da(C, 2 * C)
-        expert_product(C, 2 * C, nc.scalar.copy)
-        scatter(C, 2 * C)
-        round_weights(3, nc.scalar.copy)
-        slope(2)
-        gated_slope(3 * C, 4 * C)
-        quantize_da(2 * C, 3 * C)
-        expert_product(2 * C, 3 * C, nc.scalar.copy)
-        scatter(2 * C, 3 * C)
-        quantize_weights(3, 1)
-        weave_product(3 * C, 4 * C)
+        finish(1, C, 480, [(2, 0, 64)])
+        gated_slope(896, 1024)
+        weave_product(768, 896)
+        quantize_weights(3, 0, K)
+        weave_product(896, 1024)
         gated_slope(1024, 1152)
         quantize_da(3 * C, 4 * C)
-        expert_product(3 * C, 4 * C, nc.scalar.copy)
-        scatter(768, 960)
-        weave_product(1024, 1152)
-        w1_last.append(keep.tile([P, K * PACK], BF16, name="da_grouped_%d" % (2 * C), align_bytes=64))
-        round_weights(4, nc.vector.tensor_copy)
-        quantize_da(1024, 1152)
-        quantize_weights(4, 1)
-        expert_product(1024, 1152, nc.scalar.copy)
-        scatter(960, 1120)
+        finish(3, 800, 4 * C, [(2, 64, K)])
         gated_slope(1152, T)
+        weave_product(1024, 1152)
         weave_product(1152, T)
-        quantize_da(1152, T)
-        expert_product(1152, T, nc.vector.tensor_copy)
-        nc.vector.tensor_copy(out_sb[:].indirect(offsets[:, 1120 // PER_COL : T // PER_COL]), dx_tail[:, 1120 - 3 * C : 2 * C])
+        quantize_weights(4, 0, K)
+        quantize_weights(2, 0, 64)
+        quantize_da(4 * C, T)
+        finish(4, 4 * C, T, [])
+        gather_gated(3, 2 * C, EARLY)
+        gather_gated(0, EARLY, 3 * C)
+        quantize_weights(2, 64, K)
+        slope_product(512, 640)
+        gather_gated(1, EARLY, 3 * C)
+        gather_gated(2, EARLY, 3 * C)
+        gather_gated(3, EARLY, 3 * C)
+        quantize_da(512, 640)
+        expert_product(512, 640, nc.scalar.copy)
+        slope_product(640, 768)
+        scatter(480, 640)
+        quantize_da(640, 768)
+        expert_product(640, 768, nc.vector.tensor_copy)
+        nc.vector.tensor_copy(out_sb[:].indirect(slots(640, 800)), dx[:, 640:800])
         nc.sync.dma_start(out=out, in_=out_sb[:])

@@ -21,10 +21,9 @@ PACK = 4
 PER_COL = 16
 HALF = C // 2
 ROW_PAD = 10
-EARLY = 2 * C + HALF
+EARLY = 2 * C
 PITCH = EARLY + 6
-FIRST_TOKENS = 768
-TOKEN_CUTS = ((0, 512), (512, FIRST_TOKENS), (FIRST_TOKENS, T))
+TOKEN_CUTS = ((0, 512), (512, 1024), (1024, T))
 
 
 def tile_moe_sdb_relu2_kernel(tc, dy_words, dy_scales, w2t_words, w2t_scales, w1t, a, gate, offs, out):
@@ -54,7 +53,7 @@ def tile_moe_sdb_relu2_kernel(tc, dy_words, dy_scales, w2t_words, w2t_scales, w1
             nc.sync.dma_start(out=dy_codes[:, lo:hi].bitcast(I32), in_=words[:, lo:hi])
 
         def load_gate(lo, hi):
-            rows = keep.tile([P, hi - lo], F32, name="gate_%d" % lo)
+            rows = keep.tile([P, hi - lo], F32, name="gate_%d" % lo, align_bytes=64)
             nc.sync.dma_start(out=rows[:], in_=gate[:, lo:hi])
             for first in range(lo, hi, HALF):
                 gate_sb[first] = rows[:, first - lo :]
@@ -75,17 +74,18 @@ def tile_moe_sdb_relu2_kernel(tc, dy_words, dy_scales, w2t_words, w2t_scales, w1
         nc.gpsimd.memset(w2_plane_in[:].bitcast(I32), 0)
         load_scale_rows(w2_rows, w2t_scales)
         nc.sync.dma_start(out=w2_codes_in[:].bitcast(I32), in_=w2t_words[0].bitcast(I32))
-        load_tokens(0, FIRST_TOKENS)
+        load_tokens(0, T)
         load_scale_rows(dy_plane[:].bitcast(I32), dy_scales)
-        load_tokens(FIRST_TOKENS, T)
         load_w1(0, 1)
         load_w1(1, 1)
         load_gate(0, EARLY)
         nc.sync.dma_start(offsets[:], offs)
+        load_w1(3, 1)
         load_a(0, 2 * C)
-        load_w1(2, 3)
         load_gate(EARLY, T)
         load_a(3 * C, T)
+        load_w1(4, 1)
+        load_w1(2, 1)
         load_a(2 * C, 3 * C)
 
         for q in range(0, P, 32):
@@ -105,7 +105,6 @@ def tile_moe_sdb_relu2_kernel(tc, dy_words, dy_scales, w2t_words, w2t_scales, w1
         out_sb = keep.tile([P, T], F32)
         dx = keep.tile([P, T], F32)
         work = keep.tile([P, PACK, PITCH], F32, align_bytes=64)
-        factor = keep.tile([P, PACK, C], F32, align_bytes=64)
         grouped = {}
         da_codes = {}
         w1_rounded = {}
@@ -224,8 +223,10 @@ def tile_moe_sdb_relu2_kernel(tc, dy_words, dy_scales, w2t_words, w2t_scales, w1
         for e in range(2):
             quantize_weights(e, 0, K)
         gather_gated(0, 0, EARLY)
+        round_weights(3, 0, K, nc.vector.tensor_copy, "w1_rounded_3")
         window(1)
         gather_gated(1, 0, EARLY)
+        quantize_weights(3, 0, K)
         window(2)
         gather_gated(2, 0, EARLY)
         window(3)
@@ -235,16 +236,15 @@ def tile_moe_sdb_relu2_kernel(tc, dy_words, dy_scales, w2t_words, w2t_scales, w1
         gather_gated(3, 0, C)
         gather_gated(3, C, 2 * C)
         slope_product(0, C)
+        factor = keep.tile([P, PACK, C], F32, name="gate_0", align_bytes=64)
         gated_slope(768, 896)
         quantize_da(0, C)
         finish(0, 0, C, [(4, 0, K)])
         slope_product(C, 2 * C)
-        round_weights(3, 0, K, nc.vector.tensor_copy, "da_values_0")
+        gated_slope(896, 1024)
         quantize_da(C, 2 * C)
         finish(1, C, 480, [(2, 0, 64)])
-        gated_slope(896, 1024)
         weave_product(768, 896)
-        quantize_weights(3, 0, K)
         weave_product(896, 1024)
         gated_slope(1024, 1152)
         quantize_da(3 * C, 4 * C)
@@ -256,13 +256,14 @@ def tile_moe_sdb_relu2_kernel(tc, dy_words, dy_scales, w2t_words, w2t_scales, w1
         quantize_weights(2, 0, 64)
         quantize_da(4 * C, T)
         finish(4, 4 * C, T, [])
-        gather_gated(3, 2 * C, EARLY)
-        gather_gated(0, EARLY, 3 * C)
+        for t in range(PACK):
+            gather_gated(t, 512, 640)
+        gather_gated(0, 640, 768)
         quantize_weights(2, 64, K)
         slope_product(512, 640)
-        gather_gated(1, EARLY, 3 * C)
-        gather_gated(2, EARLY, 3 * C)
-        gather_gated(3, EARLY, 3 * C)
+        gather_gated(1, 640, 768)
+        gather_gated(2, 640, 768)
+        gather_gated(3, 640, 768)
         quantize_da(512, 640)
         expert_product(512, 640, nc.scalar.copy)
         slope_product(640, 768)

@@ -21,7 +21,7 @@ PACK = 4
 PER_COL = 16
 HALF = C // 2
 ROW_PAD = 10
-EARLY = 2 * C
+EARLY = 2 * C + HALF
 PITCH = EARLY + 6
 TOKEN_CUTS = ((0, 512), (512, 1024), (1024, T))
 
@@ -66,7 +66,7 @@ def tile_moe_sdb_relu2_kernel(tc, dy_words, dy_scales, w2t_words, w2t_scales, w1
                 a_sb[first] = rows[:, :, first - lo :]
 
         def load_w1(e0, count):
-            rows = keep.tile([P, count, PACK, K], F32, name="w1_raw_%d" % e0)
+            rows = keep.tile([P, count, PACK, K], F32, name="w1_raw_%d" % e0, align_bytes=64)
             nc.sync.dma_start(out=rows[:], in_=w1t[e0 : e0 + count].rearrange("e (p j) k -> p e j k", j=PACK))
             for e in range(count):
                 w1_raw[e0 + e] = rows[:, e, :, :]
@@ -76,15 +76,15 @@ def tile_moe_sdb_relu2_kernel(tc, dy_words, dy_scales, w2t_words, w2t_scales, w1
         nc.sync.dma_start(out=w2_codes_in[:].bitcast(I32), in_=w2t_words[0].bitcast(I32))
         load_tokens(0, T)
         load_scale_rows(dy_plane[:].bitcast(I32), dy_scales)
-        load_w1(0, 1)
-        load_w1(1, 1)
+        load_w1(0, 2)
+        load_w1(3, 1)
         load_gate(0, EARLY)
         nc.sync.dma_start(offsets[:], offs)
-        load_w1(3, 1)
         load_a(0, 2 * C)
-        load_gate(EARLY, T)
-        load_a(3 * C, T)
+        load_gate(2 * C, T)
+        load_a(3 * C, 4 * C)
         load_w1(4, 1)
+        load_a(4 * C, T)
         load_w1(2, 1)
         load_a(2 * C, 3 * C)
 
@@ -133,10 +133,11 @@ def tile_moe_sdb_relu2_kernel(tc, dy_words, dy_scales, w2t_words, w2t_scales, w1
             return work[:, :, lo - base : hi - base]
 
         def da_values(lo, hi):
-            e = lo // C
-            if e not in grouped:
-                grouped[e] = keep.tile([P, C * PACK], BF16, name="da_values_%d" % e, align_bytes=64)
-            return grouped[e][:, (lo - e * C) * PACK : (hi - e * C) * PACK]
+            first = EARLY if lo == EARLY else lo // C * C
+            if first not in grouped:
+                home = "w1_raw_2" if first == EARLY else "da_values_%d" % first
+                grouped[first] = keep.tile([P, C * PACK], BF16, name=home, align_bytes=64)
+            return grouped[first][:, (lo - first) * PACK : (hi - first) * PACK]
 
         def gather_gated(t, lo, hi):
             nc.vector.tensor_tensor(gated_rows(lo, hi)[:, t, :], dc[t][:].indirect(slots(lo, hi)), gate_sb[lo][:, 0 : hi - lo], ALU.mult)
@@ -173,7 +174,7 @@ def tile_moe_sdb_relu2_kernel(tc, dy_words, dy_scales, w2t_words, w2t_scales, w1
             )
 
         def quantize_da(lo, hi):
-            codes = keep.tile([P, hi - lo], U32, name="da_codes_%d" % lo, align_bytes=64)
+            codes = keep.tile([P, hi - lo], U32, name="da_codes_%d" % (lo if lo != EARLY else 2 * C), align_bytes=64)
             plane = keep.tile([P, hi - lo], U8, name="da_plane_%d" % lo, align_bytes=64)
             nc.vector.quantize_mx(out=codes[:].bitcast(FP8X4), scales=plane[:], in_=da_values(lo, hi))
             da_codes[lo] = (codes, plane)
@@ -188,7 +189,7 @@ def tile_moe_sdb_relu2_kernel(tc, dy_words, dy_scales, w2t_words, w2t_scales, w1
 
         def quantize_weights(e, lo, hi):
             if e not in w1_codes:
-                codes = keep.tile([P, K], U32, name="w1_codes_%d" % e, align_bytes=64)
+                codes = keep.tile([P, K], U32, name="w1_codes_%d" % (e if e != 3 else 0), align_bytes=64)
                 plane = keep.tile([P, K], U8, name="w1_plane_%d" % e, align_bytes=64)
                 w1_codes[e] = (codes, plane)
             codes, plane = w1_codes[e]
@@ -226,7 +227,6 @@ def tile_moe_sdb_relu2_kernel(tc, dy_words, dy_scales, w2t_words, w2t_scales, w1
         round_weights(3, 0, K, nc.vector.tensor_copy, "w1_rounded_3")
         window(1)
         gather_gated(1, 0, EARLY)
-        quantize_weights(3, 0, K)
         window(2)
         gather_gated(2, 0, EARLY)
         window(3)
@@ -239,34 +239,35 @@ def tile_moe_sdb_relu2_kernel(tc, dy_words, dy_scales, w2t_words, w2t_scales, w1
         factor = keep.tile([P, PACK, C], F32, name="gate_0", align_bytes=64)
         gated_slope(768, 896)
         quantize_da(0, C)
-        finish(0, 0, C, [(4, 0, K)])
+        finish(0, 0, C, [(4, 0, 64)])
         slope_product(C, 2 * C)
         gated_slope(896, 1024)
         quantize_da(C, 2 * C)
-        finish(1, C, 480, [(2, 0, 64)])
+        finish(1, C, 480, [(4, 64, K)])
         weave_product(768, 896)
+        quantize_weights(3, 0, K)
         weave_product(896, 1024)
         gated_slope(1024, 1152)
         quantize_da(3 * C, 4 * C)
-        finish(3, 800, 4 * C, [(2, 64, K)])
+        finish(3, 800, 4 * C, [(2, 0, 64)])
         gated_slope(1152, T)
         weave_product(1024, 1152)
         weave_product(1152, T)
-        quantize_weights(4, 0, K)
-        quantize_weights(2, 0, 64)
+        quantize_weights(4, 0, 64)
+        quantize_weights(4, 64, K)
         quantize_da(4 * C, T)
-        finish(4, 4 * C, T, [])
-        for t in range(PACK):
-            gather_gated(t, 512, 640)
+        finish(4, 4 * C, T, [(2, 64, K)])
+        gather_gated(3, 512, 640)
         gather_gated(0, 640, 768)
-        quantize_weights(2, 64, K)
+        quantize_weights(2, 0, 64)
         slope_product(512, 640)
         gather_gated(1, 640, 768)
         gather_gated(2, 640, 768)
         gather_gated(3, 640, 768)
         quantize_da(512, 640)
-        expert_product(512, 640, nc.scalar.copy)
+        quantize_weights(2, 64, K)
         slope_product(640, 768)
+        expert_product(512, 640, nc.vector.tensor_copy)
         scatter(480, 640)
         quantize_da(640, 768)
         expert_product(640, 768, nc.vector.tensor_copy)

@@ -20,10 +20,12 @@ P = 128
 PACK = 4
 PER_COL = 16
 HALF = C // 2
+QUARTER = C // 4
 ROW_PAD = 10
 EARLY = 2 * C + HALF
 PITCH = EARLY + 6
-TOKEN_CUTS = ((0, 512), (512, 1024), (1024, T))
+FINE_CUTS = tuple((lo, lo + C) for lo in range(0, T, C))
+WIDE_CUTS = ((0, 512), (512, 1024), (1024, T))
 
 
 def tile_moe_sdb_relu2_kernel(tc, dy_words, dy_scales, w2t_words, w2t_scales, w1t, a, gate, offs, out):
@@ -55,14 +57,14 @@ def tile_moe_sdb_relu2_kernel(tc, dy_words, dy_scales, w2t_words, w2t_scales, w1
         def load_gate(lo, hi):
             rows = keep.tile([P, hi - lo], F32, name="gate_%d" % lo, align_bytes=64)
             nc.sync.dma_start(out=rows[:], in_=gate[:, lo:hi])
-            for first in range(lo, hi, HALF):
+            for first in range(lo, hi, QUARTER):
                 gate_sb[first] = rows[:, first - lo :]
 
         def load_a(lo, hi):
             padded = keep.tile([P, PACK, hi - lo + ROW_PAD], F32, name="a_%d" % lo)
             rows = padded[:, :, 0 : hi - lo]
             nc.sync.dma_start(out=rows, in_=a[:, lo:hi].rearrange("(p t) j -> p t j", t=PACK))
-            for first in range(lo, hi, HALF):
+            for first in range(lo, hi, QUARTER):
                 a_sb[first] = rows[:, :, first - lo :]
 
         def load_w1(e0, count):
@@ -72,6 +74,8 @@ def tile_moe_sdb_relu2_kernel(tc, dy_words, dy_scales, w2t_words, w2t_scales, w1
                 w1_raw[e0 + e] = rows[:, e, :, :]
 
         nc.gpsimd.memset(w2_plane_in[:].bitcast(I32), 0)
+        zeros = keep.tile([P, HALF], F32)
+        nc.gpsimd.memset(zeros[:], 0.0)
         load_scale_rows(w2_rows, w2t_scales)
         nc.sync.dma_start(out=w2_codes_in[:].bitcast(I32), in_=w2t_words[0].bitcast(I32))
         load_tokens(0, T)
@@ -110,10 +114,12 @@ def tile_moe_sdb_relu2_kernel(tc, dy_words, dy_scales, w2t_words, w2t_scales, w1
         w1_rounded = {}
         w1_codes = {}
         products = []
+        passes = []
 
         def window(t):
-            for c, (lo, hi) in enumerate(TOKEN_CUTS):
-                bank = banks[(3 * t + c) % 6][:, 0 : hi - lo]
+            for lo, hi in FINE_CUTS if t < 2 else WIDE_CUTS:
+                bank = banks[len(passes) % 8][:, 0 : hi - lo]
+                passes.append(lo)
                 nc.tensor.matmul_mx(
                     out=bank,
                     lhsT=w2_codes[:, 2 * P * t : 2 * P * (t + 1)].bitcast(FP4X4),
@@ -237,19 +243,19 @@ def tile_moe_sdb_relu2_kernel(tc, dy_words, dy_scales, w2t_words, w2t_scales, w1
         gather_gated(3, C, 2 * C)
         slope_product(0, C)
         factor = keep.tile([P, PACK, C], F32, name="gate_0", align_bytes=64)
-        gated_slope(768, 896)
+        gated_slope(768, 832)
         quantize_da(0, C)
         finish(0, 0, C, [(4, 0, 64)])
         slope_product(C, 2 * C)
-        gated_slope(896, 1024)
+        gated_slope(832, 1024)
         quantize_da(C, 2 * C)
-        finish(1, C, 480, [(4, 64, K)])
+        finish(1, C, 2 * C, [(4, 64, K)])
         weave_product(768, 896)
         quantize_weights(3, 0, K)
         weave_product(896, 1024)
         gated_slope(1024, 1152)
         quantize_da(3 * C, 4 * C)
-        finish(3, 800, 4 * C, [(2, 0, 64)])
+        finish(3, 3 * C, 4 * C, [(2, 0, 64)])
         gated_slope(1152, T)
         weave_product(1024, 1152)
         weave_product(1152, T)
@@ -268,8 +274,8 @@ def tile_moe_sdb_relu2_kernel(tc, dy_words, dy_scales, w2t_words, w2t_scales, w1
         quantize_weights(2, 64, K)
         slope_product(640, 768)
         expert_product(512, 640, nc.vector.tensor_copy)
-        scatter(480, 640)
         quantize_da(640, 768)
-        expert_product(640, 768, nc.vector.tensor_copy)
-        nc.vector.tensor_copy(out_sb[:].indirect(slots(640, 800)), dx[:, 640:800])
+        expert_product(640, 768, nc.scalar.copy)
+        for lo in (2 * C, EARLY):
+            nc.vector.tensor_tensor(out_sb[:].indirect(slots(lo, lo + HALF)), dx[:, lo : lo + HALF], zeros[:], ALU.add)
         nc.sync.dma_start(out=out, in_=out_sb[:])

@@ -84,12 +84,14 @@ def tile_moe_sdb_relu2_kernel(tc, dy_words, dy_scales, w2t_words, w2t_scales, w1
         load_w1(3, 1)
         load_gate(0, EARLY)
         nc.sync.dma_start(offsets[:], offs)
-        load_a(0, 2 * C)
-        load_gate(2 * C, T)
+        load_a(0, C)
+        load_gate(3 * C, T)
         load_a(3 * C, 4 * C)
+        load_a(C, 2 * C)
         load_w1(4, 1)
         load_a(4 * C, T)
         load_w1(2, 1)
+        load_gate(2 * C, 3 * C)
         load_a(2 * C, 3 * C)
 
         for q in range(0, P, 32):

@@ -161,7 +161,11 @@ def tile_moe_sdb_relu2_kernel(tc, dy_words, dy_scales, w2t_words, w2t_scales, w1
             )
 
         def gather_plain(t, lo, hi):
-            nc.scalar.activation(picked[:, t, lo - 3 * C : hi - 3 * C], dc[t][:].indirect(slots(lo, hi)), ACT.Copy)
+            nc.scalar.activation(picked[:, t, lo - EARLY : hi - EARLY], dc[t][:].indirect(slots(lo, hi)), ACT.Copy)
+
+        def apply_gate(t0, lo, hi):
+            spread = gate_sb[lo][:, 0 : hi - lo].unsqueeze(1).to_broadcast([P, PACK - t0, hi - lo])
+            nc.vector.tensor_tensor(gated_rows(lo, hi)[:, t0:, :], picked[:, t0:, lo - EARLY : hi - EARLY], spread, ALU.mult)
 
         def gated_slope(lo, hi):
             nc.vector.scalar_tensor_tensor(
@@ -176,7 +180,7 @@ def tile_moe_sdb_relu2_kernel(tc, dy_words, dy_scales, w2t_words, w2t_scales, w1
         def weave_product(lo, hi):
             nc.vector.tensor_tensor(
                 out=da_values(lo, hi).rearrange("p (c i t) -> p c t i", i=2, t=PACK),
-                in0=picked[:, :, lo - 3 * C : hi - 3 * C].rearrange("p t (c i) -> p c t i", i=2),
+                in0=picked[:, :, lo - EARLY : hi - EARLY].rearrange("p t (c i) -> p c t i", i=2),
                 in1=factor[:, :, lo % C : lo % C + hi - lo].rearrange("p t (c i) -> p c t i", i=2),
                 op=ALU.mult,
             )
@@ -238,9 +242,9 @@ def tile_moe_sdb_relu2_kernel(tc, dy_words, dy_scales, w2t_words, w2t_scales, w1
         window(2)
         gather_gated(2, 0, EARLY)
         window(3)
-        picked = keep.tile([P, PACK, 2 * C], F32, align_bytes=64, tag="tokens")
+        picked = keep.tile([P, PACK, T - EARLY], F32, align_bytes=64, tag="tokens")
         for t in range(PACK):
-            gather_plain(t, 3 * C, T)
+            gather_plain(t, 3 * C if t < 2 else EARLY, T)
         gather_gated(3, 0, C)
         gather_gated(3, C, 2 * C)
         slope_product(0, C)
@@ -270,8 +274,7 @@ def tile_moe_sdb_relu2_kernel(tc, dy_words, dy_scales, w2t_words, w2t_scales, w1
         quantize_weights(2, 0, 64)
         slope_product(512, 640)
         gather_gated(1, 640, 768)
-        gather_gated(2, 640, 768)
-        gather_gated(3, 640, 768)
+        apply_gate(2, 640, 768)
         quantize_da(512, 640)
         quantize_weights(2, 64, K)
         slope_product(640, 768)

@@ -240,7 +240,7 @@ def tile_moe_sdb_relu2_kernel(tc, dy_words, dy_scales, w2t_words, w2t_scales, w1
         window(1)
         gather_gated(1, 0, EARLY)
         window(2)
-        gather_gated(2, 0, EARLY)
+        gather_gated(2, 0, 2 * C)
         window(3)
         picked = keep.tile([P, PACK, T - EARLY], F32, align_bytes=64, tag="tokens")
         for t in range(PACK):
@@ -269,6 +269,7 @@ def tile_moe_sdb_relu2_kernel(tc, dy_words, dy_scales, w2t_words, w2t_scales, w1
         quantize_weights(4, 64, K)
         quantize_da(4 * C, T)
         finish(4, 4 * C, T, [(2, 64, K)])
+        gather_gated(2, 512, 640)
         gather_gated(3, 512, 640)
         gather_gated(0, 640, 768)
         quantize_weights(2, 0, 64)

from contextlib import ExitStack

import concourse.mybir as mybir

K, T, E, C, H, N = 128, 1280, 5, 256, 512, 512
FLOPS = 2 * N * H * T + 2 * H * K * E * C

F32 = mybir.dt.float32
BF16 = mybir.dt.bfloat16
I32 = mybir.dt.int32
U32 = mybir.dt.uint32
U16 = mybir.dt.uint16
U8 = mybir.dt.uint8
FP8X4 = mybir.dt.float8_e4m3fn_x4
FP4X4 = mybir.dt.float4_e2m1fn_x4
ACT = mybir.ActivationFunctionType
ALU = mybir.AluOpType

P = 128
PACK = 4
PER_COL = 16
HALF = C // 2
QUARTER = C // 4
ROW_PAD = 10
EARLY = 2 * C + HALF
PITCH = EARLY + 6
FINE_CUTS = tuple((lo, lo + C) for lo in range(0, T, C))
WIDE_CUTS = ((0, 512), (512, 1024), (1024, T))


def tile_moe_sdb_relu2_kernel(tc, dy_words, dy_scales, w2t_words, w2t_scales, w1t, a, gate, offs, out):
    nc = tc.nc
    with ExitStack() as ctx:
        keep = ctx.enter_context(tc.tile_pool(name="keep", bufs=1))
        psum = ctx.enter_context(tc.psum_pool(name="psum", bufs=1))

        offsets = keep.tile([P, T // PER_COL], U16, name="offsets")
        dy_codes = keep.tile([P, T], U32, align_bytes=64, tag="tokens")
        dy_plane = keep.tile([P, T], U8, align_bytes=64)
        w2_codes_in = keep.tile([P, 2 * H], U8, align_bytes=64)
        w2_plane_in = keep.tile([P, H], U8, align_bytes=64)
        w2_codes = keep.tile([P, 2 * H], U8, align_bytes=64)
        w2_plane = keep.tile([P, H], U8, align_bytes=64)
        w2_rows = keep.tile([P, H // 4], I32)
        gate_sb = {}
        a_sb = {}
        w1_raw = {}

        def load_scale_rows(plane, scales):
            for r in range(4):
                nc.sync.dma_start(out=plane[r:P:32, :], in_=scales[0].bitcast(I32)[r:16:4, :])

        def load_tokens(lo, hi):
            words = dy_words[0].rearrange("p t d -> p (t d)").bitcast(I32)
            nc.sync.dma_start(out=dy_codes[:, lo:hi].bitcast(I32), in_=words[:, lo:hi])

        def load_gate(lo, hi):
            rows = keep.tile([P, hi - lo], F32, name="gate_%d" % lo, align_bytes=64)
            nc.sync.dma_start(out=rows[:], in_=gate[:, lo:hi])
            for first in range(lo, hi, QUARTER):
                gate_sb[first] = rows[:, first - lo :]

        def load_a(lo, hi):
            padded = keep.tile([P, PACK, hi - lo + ROW_PAD], F32, name="a_%d" % lo)
            rows = padded[:, :, 0 : hi - lo]
            nc.sync.dma_start(out=rows, in_=a[:, lo:hi].rearrange("(p t) j -> p t j", t=PACK))
            for first in range(lo, hi, QUARTER):
                a_sb[first] = rows[:, :, first - lo :]

        def load_w1(e0, count):
            rows = keep.tile([P, count, PACK, K], F32, name="w1_raw_%d" % e0, align_bytes=64)
            nc.sync.dma_start(out=rows[:], in_=w1t[e0 : e0 + count].rearrange("e (p j) k -> p e j k", j=PACK))
            for e in range(count):
                w1_raw[e0 + e] = rows[:, e, :, :]

        nc.gpsimd.memset(w2_plane_in[:].bitcast(I32), 0)
        zeros = keep.tile([P, HALF], F32)
        nc.gpsimd.memset(zeros[:], 0.0)
        load_scale_rows(w2_rows, w2t_scales)
        nc.sync.dma_start(out=w2_codes_in[:].bitcast(I32), in_=w2t_words[0].bitcast(I32))
        load_tokens(0, T)
        load_scale_rows(dy_plane[:].bitcast(I32), dy_scales)
        load_w1(0, 2)
        load_w1(3, 1)
        load_gate(0, EARLY)
        nc.sync.dma_start(offsets[:], offs)
        load_a(0, C)
        load_gate(3 * C, T)
        load_a(3 * C, 4 * C)
        load_a(C, 2 * C)
        load_w1(4, 1)
        load_a(4 * C, T)
        load_w1(2, 1)
        load_gate(2 * C, 3 * C)
        load_a(2 * C, 3 * C)

        for q in range(0, P, 32):
            nc.vector.tensor_copy(out=w2_plane_in[:].bitcast(I32)[q : q + 4, :], in_=w2_rows[q : q + 4, :])
        for ts in (slice(0, 1), slice(1, PACK)):
            nc.vector.tensor_copy(
                out=w2_codes[:].bitcast(U16).rearrange("p (t m) -> p t m", t=PACK)[:, ts, :],
                in_=w2_codes_in[:].bitcast(U16).rearrange("p (m t) -> p t m", t=PACK)[:, ts, :],
            )
            nc.vector.tensor_copy(
                out=w2_plane[:].rearrange("p (t m) -> p t m", t=PACK)[:, ts, :],
                in_=w2_plane_in[:].rearrange("p (m t) -> p t m", t=PACK)[:, ts, :],
            )

        banks = [psum.tile([P, 512], F32, name="bank_%d" % n) for n in range(8)]
        dc = [keep.tile([P, T], F32, name="dc_%d" % t) for t in range(PACK)]
        out_sb = keep.tile([P, T], F32)
        dx = keep.tile([P, T], F32)
        work = keep.tile([P, PACK, PITCH], F32, align_bytes=64)
        grouped = {}
        da_codes = {}
        w1_rounded = {}
        w1_codes = {}
        products = []
        passes = []

        def window(t):
            for lo, hi in FINE_CUTS if t < 2 else WIDE_CUTS:
                bank = banks[len(passes) % 8][:, 0 : hi - lo]
                passes.append(lo)
                nc.tensor.matmul_mx(
                    out=bank,
                    lhsT=w2_codes[:, 2 * P * t : 2 * P * (t + 1)].bitcast(FP4X4),
                    lhsT_scale=w2_plane[:, P * t : P * (t + 1)],
                    rhs=dy_codes[:, lo:hi].bitcast(FP8X4),
                    rhs_scale=dy_plane[:, lo:hi],
                    start=True,
                    stop=True,
                )
                nc.scalar.activation(out=dc[t][:, lo:hi], in_=bank, func=ACT.Copy, scale=2.0)

        def slots(lo, hi):
            return offsets[:, lo // PER_COL : hi // PER_COL]

        def gated_rows(lo, hi):
            base = 0 if lo < EARLY else EARLY
            return work[:, :, lo - base : hi - base]

        def da_values(lo, hi):
            first = EARLY if lo == EARLY else lo // C * C
            if first not in grouped:
                home = "w1_raw_2" if first == EARLY else "da_values_%d" % first
                grouped[first] = keep.tile([P, C * PACK], BF16, name=home, align_bytes=64)
            return grouped[first][:, (lo - first) * PACK : (hi - first) * PACK]

        def gather_gated(t, lo, hi):
            nc.vector.tensor_tensor(gated_rows(lo, hi)[:, t, :], dc[t][:].indirect(slots(lo, hi)), gate_sb[lo][:, 0 : hi - lo], ALU.mult)

        def slope_product(lo, hi):
            nc.vector.scalar_tensor_tensor(
                out=da_values(lo, hi).rearrange("p (s t) -> p s t", t=PACK),
                in0=a_sb[lo][:, :, 0 : hi - lo].rearrange("p t s -> p s t"),
                scalar=0.0,
                in1=gated_rows(lo, hi).rearrange("p t s -> p s t"),
                op0=ALU.max,
                op1=ALU.mult,
            )

        def gather_plain(t, lo, hi):
            nc.scalar.activation(picked[:, t, lo - EARLY : hi - EARLY], dc[t][:].indirect(slots(lo, hi)), ACT.Copy)

        def apply_gate(t0, lo, hi):
            spread = gate_sb[lo][:, 0 : hi - lo].unsqueeze(1).to_broadcast([P, PACK - t0, hi - lo])
            nc.vector.tensor_tensor(gated_rows(lo, hi)[:, t0:, :], picked[:, t0:, lo - EARLY : hi - EARLY], spread, ALU.mult)

        def gated_slope(lo, hi):
            nc.vector.scalar_tensor_tensor(
                out=factor[:, :, lo % C : lo % C + hi - lo],
                in0=a_sb[lo][:, :, 0 : hi - lo],
                scalar=0.0,
                in1=gate_sb[lo][:, 0 : hi - lo].unsqueeze(1).to_broadcast([P, PACK, hi - lo]),
                op0=ALU.max,
                op1=ALU.mult,
            )

        def weave_product(lo, hi):
            nc.vector.tensor_tensor(
                out=da_values(lo, hi).rearrange("p (c i t) -> p c t i", i=2, t=PACK),
                in0=picked[:, :, lo - EARLY : hi - EARLY].rearrange("p t (c i) -> p c t i", i=2),
                in1=factor[:, :, lo % C : lo % C + hi - lo].rearrange("p t (c i) -> p c t i", i=2),
                op=ALU.mult,
            )

        def quantize_da(lo, hi):
            codes = keep.tile([P, hi - lo], U32, name="da_codes_%d" % (lo if lo != EARLY else 2 * C), align_bytes=64)
            plane = keep.tile([P, hi - lo], U8, name="da_plane_%d" % lo, align_bytes=64)
            nc.vector.quantize_mx(out=codes[:].bitcast(FP8X4), scales=plane[:], in_=da_values(lo, hi))
            da_codes[lo] = (codes, plane)

        def round_weights(e, lo, hi, engine_copy, home):
            rounded = keep.tile([P, (hi - lo) * PACK], BF16, name=home, align_bytes=64)
            engine_copy(
                out=rounded[:].rearrange("p (c i j) -> p c j i", i=4, j=PACK),
                in_=w1_raw[e][:, :, lo:hi].rearrange("p j (c i) -> p c j i", i=4),
            )
            w1_rounded[e, lo] = rounded

        def quantize_weights(e, lo, hi):
            if e not in w1_codes:
                codes = keep.tile([P, K], U32, name="w1_codes_%d" % (e if e != 3 else 0), align_bytes=64)
                plane = keep.tile([P, K], U8, name="w1_plane_%d" % e, align_bytes=64)
                w1_codes[e] = (codes, plane)
            codes, plane = w1_codes[e]
            nc.vector.quantize_mx(out=codes[:, lo:hi].bitcast(FP8X4), scales=plane[:, lo:hi], in_=w1_rounded[e, lo][:])

        def expert_product(lo, hi, engine_copy):
            acc = banks[6 + len(products) % 2][:, 0 : hi - lo]
            products.append(lo)
            nc.tensor.matmul_mx(
                out=acc,
                lhsT=w1_codes[lo // C][0][:].bitcast(FP8X4),
                lhsT_scale=w1_codes[lo // C][1][:],
                rhs=da_codes[lo][0][:].bitcast(FP8X4),
                rhs_scale=da_codes[lo][1][:],
                start=True,
                stop=True,
            )
            engine_copy(out=dx[:, lo:hi], in_=acc)

        def scatter(lo, hi):
            nc.scalar.activation(out_sb[:].indirect(slots(lo, hi)), dx[:, lo:hi], ACT.Copy)

        def finish(e, lo, hi, late):
            expert_product(e * C, (e + 1) * C, nc.scalar.copy)
            for args in late:
                round_weights(*args, nc.scalar.copy, "da_codes_%d" % (e * C))
            scatter(lo, hi)

        window(0)
        for e in range(2):
            round_weights(e, 0, K, nc.vector.tensor_copy, "w1_rounded_%d" % e)
        for e in range(2):
            quantize_weights(e, 0, K)
        gather_gated(0, 0, EARLY)
        round_weights(3, 0, K, nc.vector.tensor_copy, "w1_rounded_3")
        window(1)
        gather_gated(1, 0, EARLY)
        window(2)
        gather_gated(2, 0, 2 * C)
        window(3)
        picked = keep.tile([P, PACK, T - EARLY], F32, align_bytes=64, tag="tokens")
        for t in range(PACK):
            gather_plain(t, 3 * C if t < 2 else EARLY, T)
        gather_gated(3, 0, C)
        gather_gated(3, C, 2 * C)
        slope_product(0, C)
        factor = keep.tile([P, PACK, C], F32, name="gate_0", align_bytes=64)
        gated_slope(768, 832)
        quantize_da(0, C)
        finish(0, 0, C, [(4, 0, 64)])
        slope_product(C, 2 * C)
        gated_slope(832, 1024)
        quantize_da(C, 2 * C)
        finish(1, C, 2 * C, [(4, 64, K)])
        weave_product(768, 896)
        quantize_weights(3, 0, K)
        weave_product(896, 1024)
        gated_slope(1024, 1152)
        quantize_da(3 * C, 4 * C)
        finish(3, 3 * C, 4 * C, [(2, 0, 64)])
        gated_slope(1152, T)
        weave_product(1024, 1152)
        weave_product(1152, T)
        quantize_weights(4, 0, 64)
        quantize_weights(4, 64, K)
        quantize_da(4 * C, T)
        finish(4, 4 * C, T, [(2, 64, K)])
        gather_gated(2, 512, 640)
        gather_gated(3, 512, 640)
        gather_gated(0, 640, 768)
        quantize_weights(2, 0, 64)
        slope_product(512, 640)
        gather_gated(1, 640, 768)
        apply_gate(2, 640, 768)
        quantize_da(512, 640)
        quantize_weights(2, 64, K)
        slope_product(640, 768)
        expert_product(512, 640, nc.vector.tensor_copy)
        quantize_da(640, 768)
        expert_product(640, 768, nc.scalar.copy)
        for lo in (2 * C, EARLY):
            nc.vector.tensor_tensor(out_sb[:].indirect(slots(lo, lo + HALF)), dx[:, lo : lo + HALF], zeros[:], ALU.add)
        nc.sync.dma_start(out=out, in_=out_sb[:])
